import numpy as np
import ml_dtypes


def mxq(x, axis, fmt="e4m3"):
    dtype, down = {"e4m3": (ml_dtypes.float8_e4m3fn, 7), "e5m2": (ml_dtypes.float8_e5m2, 14)}[fmt]
    v = np.moveaxis(np.asarray(x, np.float32).astype(ml_dtypes.bfloat16).astype(np.float64), axis, -1)
    blocks = v.reshape(v.shape[:-1] + (-1, 32))
    amax = np.abs(blocks).max(-1, keepdims=True)
    byte = np.maximum(np.where(amax > 0, np.frexp(amax)[1] - 1 + 127, 0) - down, 1)
    scale = np.exp2(byte - 127.0)
    codes = (blocks / scale).astype(np.float32).astype(dtype).astype(np.float64)
    return np.moveaxis((codes * scale).reshape(v.shape), -1, axis)


WIDE = False


def mx_kscale(k):
    if not WIDE:
        return np.ones(k)
    levels = np.array([24, -24, 12, -12, 0])
    if k % 512:
        return np.exp2(np.random.permutation(np.resize(levels, k // 32))).repeat(32)
    a = np.empty((k // 512, 16))
    for p in range(k // 512):
        a[p, :8] = np.random.permutation(np.resize(levels, 8))
        for g in range(8):
            far = levels[np.abs(levels - a[p, g]) >= 10]
            a[p, g + 8] = far[np.random.randint(len(far))]
    return np.exp2(a.ravel()).repeat(32)


def f64(x):
    return np.asarray(x).astype(np.float64)


def striped(idx):
    return np.tile(idx.reshape(-1, 16).T, (8, 1)).astype(np.uint16)


def unstriped(offs):
    return offs[:16].T.reshape(-1).astype(np.int64)


E2M1 = np.array([0.0, 0.5, 1.0, 1.5, 2.0, 3.0, 4.0, 6.0, -0.0, -0.5, -1.0, -1.5, -2.0, -3.0, -4.0, -6.0])


def pack_weight(w, fmt):
    k, n = w.shape
    w = f64(np.asarray(w, np.float32).astype(ml_dtypes.bfloat16)).reshape(k // 32, 32, n)
    amax = np.abs(w).max(1)
    if fmt == "e4m3":
        byte = np.frexp(amax)[1] - 1 + 127 - 7
    else:
        mant, ex = np.frexp(amax / 6.0)
        byte = np.where(mant > 0.5, ex, ex - 1) + 127
    byte = np.clip(np.where(amax > 0, byte, 1), 1, 254)
    scaled = (w * np.exp2(127.0 - byte)[:, None, :]).reshape(k, n).astype(np.float32)
    by_word = np.ascontiguousarray(scaled.reshape(k // 512, 128, 4, n).transpose(0, 1, 3, 2))
    if fmt == "e4m3":
        words = by_word.astype(ml_dtypes.float8_e4m3fn).view(np.uint8)
    else:
        c = by_word.astype(ml_dtypes.float4_e2m1fn).view(np.uint8) & 0xF
        words = (c[..., 0::2] | (c[..., 1::2] << 4)).reshape(k // 512, 128, 2 * n)
    return np.ascontiguousarray(words), np.ascontiguousarray(byte.astype(np.uint8).reshape(k // 512, 16, n))


def unpack_weight(words, scales, fmt):
    g, _, n = scales.shape
    words = np.ascontiguousarray(words).reshape(g, 128, n, -1)
    if fmt == "e4m3":
        vals = words.view(ml_dtypes.float8_e4m3fn).astype(np.float64)
    else:
        nib = np.empty((g, 128, n, 4), np.uint8)
        nib[..., 0::2] = words & 0xF
        nib[..., 1::2] = words >> 4
        vals = E2M1[nib]
    vals = vals * np.repeat(np.exp2(scales.astype(np.float64) - 127.0), 8, axis=1)[..., None]
    return vals.transpose(0, 1, 3, 2).reshape(g * 512, n)


def pack_table4(v):
    words, scales = pack_weight(v, "e2m1")
    g, t = words.shape[0] // 2, v.shape[1]
    return np.ascontiguousarray(words.reshape(g, 2, 128, t, 2).transpose(0, 2, 3, 1, 4).reshape(g, 128, t, 4)), scales


def unpack_table4(words, scales):
    g, _, t, _ = words.shape
    return unpack_weight(words.reshape(g, 128, t, 2, 2).transpose(0, 3, 1, 2, 4).reshape(2 * g, 128, 2 * t), scales, "e2m1")


K, R, N, T, J = 1024, 512, 512, 4096, 1024


def setup_inputs():
    n = np.random.standard_normal
    s = mx_kscale(K)[:, None]
    u = mx_kscale(R)[:, None]
    p_tab = pack_table4(n((K, T)) * s)
    p_wb = pack_weight(0.7 * n((K, N)) / np.sqrt(K) / s, "e4m3")
    p_upw = pack_weight(2.0 * n((R, N)) / np.sqrt(R) / u, "e2m1")
    return {
        "tab_words": p_tab[0],
        "tab_scales": p_tab[1],
        "wb_words": p_wb[0],
        "wb_scales": p_wb[1],
        "dn": (n((K, R)) / np.sqrt(K) / s).astype(np.float32),
        "sm": (np.random.uniform(0.5, 2.0, R) * u[:, 0]).astype(np.float32),
        "upw_words": p_upw[0],
        "upw_scales": p_upw[1],
        "x0T": (n((N, T))).astype(np.float32),
        "b": (0.3 * n(N)).astype(np.float32),
        "offs": striped(np.random.permutation(T)[:J]),
    }


def reference(tab_words, tab_scales, wb_words, wb_scales, dn, sm, upw_words, upw_scales, x0T, b, offs):
    idx = unstriped(offs)
    tab_ = unpack_table4(tab_words, tab_scales)[:, idx]
    wb_ = unpack_weight(wb_words, wb_scales, "e4m3")
    dn_ = mxq(f64(dn), 0, "e4m3")
    hs = dn_.T @ tab_
    h = f64(sm)[:, None] * np.tanh(hs)
    h_ = mxq(h, 0, "e4m3")
    upw_ = unpack_weight(upw_words, upw_scales, "e2m1")
    y = wb_.T @ tab_ + upw_.T @ h_
    return f64(x0T)[:, idx] * (y + f64(b)[:, None]) + f64(x0T)[:, idx]

@@ -1,0 +1,186 @@
+from contextlib import ExitStack
+
+import concourse.mybir as mybir
+
+K, R, N, T, J = 1024, 512, 512, 4096, 1024
+FLOPS = 2 * J * (K * R + K * N + R * N)
+
+F32 = mybir.dt.float32
+BF16 = mybir.dt.bfloat16
+I32 = mybir.dt.int32
+U32 = mybir.dt.uint32
+U16 = mybir.dt.uint16
+U8 = mybir.dt.uint8
+FP8X4 = mybir.dt.float8_e4m3fn_x4
+FP4X4 = mybir.dt.float4_e2m1fn_x4
+ACT = mybir.ActivationFunctionType
+ALU = mybir.AluOpType
+
+P = 128
+PACK = 4
+PASSES = K // (P * PACK)
+HALF = 512
+HALVES = J // HALF
+CH = 128
+NT = N // P
+QUADS = 4
+
+
+def tile_list_xcross_tanh_kernel(
+    tc, tab_words, tab_scales, wb_words, wb_scales, dn, sm, upw_words, upw_scales, x0T, b, offs, out
+):
+    nc = tc.nc
+    with ExitStack() as ctx:
+        keep = ctx.enter_context(tc.tile_pool(name="keep", bufs=1))
+        ring = ctx.enter_context(tc.tile_pool(name="ring", bufs=2))
+        hs_psum = ctx.enter_context(tc.psum_pool(name="hs_psum", bufs=4))
+        y_psum = ctx.enter_context(tc.psum_pool(name="y_psum", bufs=4))
+
+        reuse = ctx.enter_context(tc.tile_pool(name="reuse", bufs=1))
+
+        offsets = keep.tile([P, J // 16], U16, name="offsets")
+        tabs = reuse.tile([P, T], U8, name="tabs", offset=0, align_bytes=64)
+        dn_raw = [keep.tile([P, PACK, R], F32, name=f"dn_raw{a}", tag=f"slot_raw{a}", align_bytes=64) for a in range(PASSES)]
+        sm_t = keep.tile([P, PACK], F32, name="sm_t")
+        b_t = keep.tile([P, NT], F32, name="b_t")
+        tabw = keep.tile([P, T], I32, name="tabw", align_bytes=64)
+        planes = keep.tile([P, PASSES * J + PASSES * N], U8, name="planes", align_bytes=64)
+
+        nc.sync.dma_start(out=tabs[96:128, :].bitcast(I32), in_=tab_scales.rearrange("a q t -> (a q) t").bitcast(I32))
+        nc.sync.dma_start(offsets[:], offs)
+        nc.scalar.dma_start(out=sm_t[:], in_=sm.rearrange("(p t) -> p t", t=PACK))
+        with nc.allow_non_contiguous_dma(reason="one bias value a partition"):
+            nc.scalar.dma_start(out=b_t[:], in_=b.rearrange("(c p) -> p c", p=P))
+        for a in range(PASSES):
+            nc.sync.dma_start(out=dn_raw[a][:], in_=dn[512 * a : 512 * (a + 1), :].rearrange("(p i) r -> p i r", i=PACK))
+
+        nc.sync.dma_start(out=tabw[:], in_=tab_words[0].rearrange("p t i -> p (t i)").bitcast(I32))
+        nc.vector.memset(tabs[0:96, :].bitcast(I32), 0)
+        nc.vector.memset(planes[:].bitcast(I32), 0)
+        v_scales = [planes[:, a * J : (a + 1) * J] for a in range(PASSES)]
+        wbs = planes[:, PASSES * J :]
+        for q in range(QUADS):
+            nc.gpsimd.dma_start(
+                out=wbs[32 * q : 32 * q + 4, :].bitcast(I32).rearrange("r (a n) -> r a n", a=PASSES),
+                in_=wb_scales[:, 4 * q : 4 * q + 4, :].bitcast(I32).rearrange("a r n -> r a n"),
+            )
+
+        picked_rows = keep.tile([P, J], U8, name="picked_rows", align_bytes=64)
+        nc.vector.tensor_copy(out=picked_rows[:], in_=tabs[:].indirect(offsets[:]))
+        upw = reuse.tile([P, 2 * N], U8, name="upw", offset=0, align_bytes=64)
+        ups = reuse.tile([P, N], U8, name="ups", offset=1024, align_bytes=64)
+        wbw = reuse.tile([P, PASSES, N], I32, name="wbw", offset=1536, align_bytes=64)
+        nc.vector.memset(ups[:].bitcast(I32), 0)
+        for a, queue in enumerate((nc.gpsimd, nc.sync)):
+            for q in range(QUADS):
+                row = 96 + 16 * a + 4 * q
+                queue.dma_start(
+                    out=v_scales[a][32 * q : 32 * q + 4, :].bitcast(I32), in_=picked_rows[row : row + 4, :].bitcast(I32)
+                )
+        nc.sync.dma_start(out=wbw[:], in_=wb_words.rearrange("a p n i -> p a (n i)").bitcast(I32))
+        nc.sync.dma_start(out=upw[:].bitcast(I32), in_=upw_words[0].bitcast(I32))
+        for q in range(QUADS):
+            nc.sync.dma_start(
+                out=ups[32 * q : 32 * q + 4, :].bitcast(I32), in_=upw_scales[0, 4 * q : 4 * q + 4, :].bitcast(I32)
+            )
+
+        b1 = keep.tile([P, NT], F32, name="b1")
+        nc.vector.tensor_scalar(out=b1[:], in0=b_t[:], scalar1=1.0, scalar2=None, op0=ALU.add)
+
+        dn_codes, dn_scales = [], []
+        for a in range(PASSES):
+            dn_bf = keep.tile([P, R * PACK], BF16, name=f"dn_bf{a}", tag=f"slot_bf{a}", align_bytes=64)
+            nc.scalar.copy(
+                out=dn_bf[:].rearrange("p (t m i) -> p m i t", t=PACK, i=PACK),
+                in_=dn_raw[a][:].rearrange("p i (m t) -> p m i t", t=PACK),
+            )
+            codes = keep.tile([P, R], U32, name=f"dn_codes{a}", align_bytes=64)
+            scales = keep.tile([P, R], U8, name=f"dn_scales{a}", align_bytes=64)
+            nc.vector.quantize_mx(out=codes[:].bitcast(FP8X4), scales=scales[:], in_=dn_bf[:])
+            dn_codes.append(codes)
+            dn_scales.append(scales)
+
+        x0 = []
+        for c, slot in enumerate(("slot_raw0", "slot_bf0", "slot_raw1", "slot_bf1")):
+            x0.append(keep.tile([P, T], F32, name=f"x0_{c}", tag=slot, align_bytes=64))
+            nc.sync.dma_start(out=x0[c][:], in_=x0T[c * P : (c + 1) * P, :])
+
+        v_codes = []
+        for hh in range(HALVES):
+            both = ring.tile([P, HALF], U32, name="both", align_bytes=64)
+            nc.vector.tensor_copy(
+                out=both[:], in_=tabw[:].bitcast(U32).indirect(offsets[:, hh * 32 : (hh + 1) * 32])
+            )
+            parted = keep.tile([P, PASSES * 2 * HALF], U8, name=f"v_codes{hh}", align_bytes=64)
+            nc.vector.tensor_copy(
+                out=parted[:].bitcast(U16).rearrange("p (a j) -> p a j", a=PASSES),
+                in_=both[:].bitcast(U16).rearrange("p (j a) -> p a j", a=PASSES),
+            )
+            v_codes.append(parted)
+
+        h_codes, h_scales = [], []
+        for hh in range(HALVES):
+            h_bf = ring.tile([P, HALF * PACK], BF16, name="h_bf", align_bytes=64)
+            for pair in range(2):
+                th = ring.tile([P, 2 * CH * PACK], F32, name="th")
+                for u in range(2):
+                    j0 = (2 * pair + u) * CH
+                    hs = hs_psum.tile([P, PACK, CH], F32, name="hs")
+                    for t in range(PACK):
+                        for a in range(PASSES):
+                            nc.tensor.matmul_mx(
+                                out=hs[:, t, :],
+                                lhsT=dn_codes[a][:, t * P : (t + 1) * P].bitcast(FP8X4),
+                                lhsT_scale=dn_scales[a][:, t * P : (t + 1) * P],
+                                rhs=v_codes[hh][:, 2 * (a * HALF + j0) : 2 * (a * HALF + j0 + CH)].bitcast(FP4X4),
+                                rhs_scale=v_scales[a][:, hh * HALF + j0 : hh * HALF + j0 + CH],
+                                start=(a == 0),
+                                stop=(a == PASSES - 1),
+                            )
+                    nc.scalar.activation(
+                        out=th[:, u * CH * PACK : (u + 1) * CH * PACK].rearrange("p (j t) -> p j t", t=PACK),
+                        in_=hs[:].rearrange("p t j -> p j t"),
+                        func=ACT.Tanh,
+                    )
+                nc.vector.tensor_tensor(
+                    out=h_bf[:, pair * 2 * CH * PACK : (pair + 1) * 2 * CH * PACK].rearrange("p (j t) -> p j t", t=PACK),
+                    in0=th[:].rearrange("p (j t) -> p j t", t=PACK),
+                    in1=sm_t[:].unsqueeze(1).to_broadcast([P, 2 * CH, PACK]),
+                    op=ALU.mult,
+                )
+            h_codes.append(keep.tile([P, HALF], U32, name=f"h_codes{hh}", align_bytes=64))
+            h_scales.append(keep.tile([P, HALF], U8, name=f"h_scales{hh}", align_bytes=64))
+            nc.vector.quantize_mx(out=h_codes[hh][:].bitcast(FP8X4), scales=h_scales[hh][:], in_=h_bf[:])
+
+        for c in range(NT):
+            for hh in range(HALVES):
+                y = y_psum.tile([P, HALF], F32, name="y")
+                for a in range(PASSES):
+                    nc.tensor.matmul_mx(
+                        out=y[:],
+                        lhsT=wbw[:, a, c * P : (c + 1) * P].bitcast(FP8X4),
+                        lhsT_scale=wbs[:, a * N + c * P : a * N + (c + 1) * P],
+                        rhs=v_codes[hh][:, 2 * a * HALF : 2 * (a + 1) * HALF].bitcast(FP4X4),
+                        rhs_scale=v_scales[a][:, hh * HALF : (hh + 1) * HALF],
+                        start=(a == 0),
+                        stop=False,
+                    )
+                nc.tensor.matmul_mx(
+                    out=y[:],
+                    lhsT=upw[:, 2 * c * P : 2 * (c + 1) * P].bitcast(FP4X4),
+                    lhsT_scale=ups[:, c * P : (c + 1) * P],
+                    rhs=h_codes[hh][:].bitcast(FP8X4),
+                    rhs_scale=h_scales[hh][:],
+                    start=False,
+                    stop=True,
+                )
+                y1 = ring.tile([P, HALF], F32, name="y1", bufs=3)
+                nc.scalar.activation(out=y1[:], in_=y[:], func=ACT.Identity, bias=b1[:, c : c + 1])
+                res = keep.tile([P, HALF], F32, name=f"res_{c}_{hh}")
+                nc.vector.tensor_tensor(
+                    out=res[:],
+                    in0=x0[c][:].indirect(offsets[:, hh * 32 : (hh + 1) * 32]),
+                    in1=y1[:],
+                    op=ALU.mult,
+                )
+                nc.sync.dma_start(out=out[c * P : (c + 1) * P, hh * HALF : (hh + 1) * HALF], in_=res[:])

@@ -1,6 +1,7 @@
 from contextlib import ExitStack
 
 import concourse.mybir as mybir
+from concourse.masks import make_identity
 
 K, R, N, T, J = 1024, 512, 512, 4096, 1024
 FLOPS = 2 * J * (K * R + K * N + R * N)
@@ -39,22 +40,21 @@ def tile_list_xcross_tanh_kernel(
         reuse = ctx.enter_context(tc.tile_pool(name="reuse", bufs=1))
 
         offsets = keep.tile([P, J // 16], U16, name="offsets")
-        tabs = reuse.tile([P, T], U8, name="tabs", offset=0, align_bytes=64)
+        tabs = reuse.tile([P, T], U8, name="tabs", offset=15872, align_bytes=64)
         dn_raw = [keep.tile([P, PACK, R], F32, name=f"dn_raw{a}", tag=f"slot_raw{a}", align_bytes=64) for a in range(PASSES)]
         sm_t = keep.tile([P, PACK], F32, name="sm_t")
-        b_t = keep.tile([P, NT], F32, name="b_t")
-        tabw = keep.tile([P, T], I32, name="tabw", align_bytes=64)
+        b_rows = keep.tile([P, P], F32, name="b_rows")
+        ident = keep.tile([P, P], F32, name="ident")
+        upw = keep.tile([P, 2 * N], U8, name="upw", align_bytes=64)
         planes = keep.tile([P, PASSES * J + PASSES * N], U8, name="planes", align_bytes=64)
 
         nc.sync.dma_start(out=tabs[96:128, :].bitcast(I32), in_=tab_scales.rearrange("a q t -> (a q) t").bitcast(I32))
         nc.sync.dma_start(offsets[:], offs)
         nc.scalar.dma_start(out=sm_t[:], in_=sm.rearrange("(p t) -> p t", t=PACK))
-        with nc.allow_non_contiguous_dma(reason="one bias value a partition"):
-            nc.scalar.dma_start(out=b_t[:], in_=b.rearrange("(c p) -> p c", p=P))
         for a in range(PASSES):
             nc.sync.dma_start(out=dn_raw[a][:], in_=dn[512 * a : 512 * (a + 1), :].rearrange("(p i) r -> p i r", i=PACK))
 
-        nc.sync.dma_start(out=tabw[:], in_=tab_words[0].rearrange("p t i -> p (t i)").bitcast(I32))
+        nc.sync.dma_start(out=upw[:].bitcast(I32), in_=upw_words[0].bitcast(I32))
         nc.vector.memset(tabs[0:96, :].bitcast(I32), 0)
         nc.vector.memset(planes[:].bitcast(I32), 0)
         v_scales = [planes[:, a * J : (a + 1) * J] for a in range(PASSES)]
@@ -65,27 +65,30 @@ def tile_list_xcross_tanh_kernel(
                 in_=wb_scales[:, 4 * q : 4 * q + 4, :].bitcast(I32).rearrange("a r n -> r a n"),
             )
 
+        nc.gpsimd.memset(b_rows[:], 0.0)
+        nc.gpsimd.dma_start(out=b_rows[0:NT, :], in_=b.rearrange("(c p) -> c p", p=P))
+        make_identity(nc, ident[:])
+
         picked_rows = keep.tile([P, J], U8, name="picked_rows", align_bytes=64)
         nc.vector.tensor_copy(out=picked_rows[:], in_=tabs[:].indirect(offsets[:]))
-        upw = reuse.tile([P, 2 * N], U8, name="upw", offset=0, align_bytes=64)
-        ups = reuse.tile([P, N], U8, name="ups", offset=1024, align_bytes=64)
-        wbw = reuse.tile([P, PASSES, N], I32, name="wbw", offset=1536, align_bytes=64)
+        tabw = reuse.tile([P, T], I32, name="tabw", offset=0, align_bytes=64)
+        ups = reuse.tile([P, N], U8, name="ups", offset=16384, align_bytes=64)
+        wbw = reuse.tile([P, PASSES, N], I32, name="wbw", offset=16896, align_bytes=64)
         nc.vector.memset(ups[:].bitcast(I32), 0)
-        for a, queue in enumerate((nc.gpsimd, nc.sync)):
+        for a in range(PASSES):
             for q in range(QUADS):
                 row = 96 + 16 * a + 4 * q
-                queue.dma_start(
+                nc.sync.dma_start(
                     out=v_scales[a][32 * q : 32 * q + 4, :].bitcast(I32), in_=picked_rows[row : row + 4, :].bitcast(I32)
                 )
+                if (a, q) == (0, 1):
+                    nc.sync.dma_start(out=tabw[:], in_=tab_words[0].rearrange("p t i -> p (t i)").bitcast(I32))
         nc.sync.dma_start(out=wbw[:], in_=wb_words.rearrange("a p n i -> p a (n i)").bitcast(I32))
-        nc.sync.dma_start(out=upw[:].bitcast(I32), in_=upw_words[0].bitcast(I32))
-        for q in range(QUADS):
-            nc.sync.dma_start(
-                out=ups[32 * q : 32 * q + 4, :].bitcast(I32), in_=upw_scales[0, 4 * q : 4 * q + 4, :].bitcast(I32)
-            )
 
         b1 = keep.tile([P, NT], F32, name="b1")
-        nc.vector.tensor_scalar(out=b1[:], in0=b_t[:], scalar1=1.0, scalar2=None, op0=ALU.add)
+        b_cols = y_psum.tile([P, HALF], F32, name="y")
+        nc.tensor.transpose(b_cols[:, 0:P], b_rows[:], ident[:])
+        nc.vector.tensor_scalar(out=b1[:], in0=b_cols[:, 0:NT], scalar1=1.0, scalar2=None, op0=ALU.add)
 
         dn_codes, dn_scales = [], []
         for a in range(PASSES):
@@ -104,6 +107,11 @@ def tile_list_xcross_tanh_kernel(
         for c, slot in enumerate(("slot_raw0", "slot_bf0", "slot_raw1", "slot_bf1")):
             x0.append(keep.tile([P, T], F32, name=f"x0_{c}", tag=slot, align_bytes=64))
             nc.sync.dma_start(out=x0[c][:], in_=x0T[c * P : (c + 1) * P, :])
+            if c == 0:
+                for q in range(QUADS):
+                    nc.sync.dma_start(
+                        out=ups[32 * q : 32 * q + 4, :].bitcast(I32), in_=upw_scales[0, 4 * q : 4 * q + 4, :].bitcast(I32)
+                    )
 
         v_codes = []
         for hh in range(HALVES):
@@ -176,11 +184,15 @@ def tile_list_xcross_tanh_kernel(
                 )
                 y1 = ring.tile([P, HALF], F32, name="y1", bufs=3)
                 nc.scalar.activation(out=y1[:], in_=y[:], func=ACT.Identity, bias=b1[:, c : c + 1])
-                res = keep.tile([P, HALF], F32, name=f"res_{c}_{hh}")
-                nc.vector.tensor_tensor(
-                    out=res[:],
-                    in0=x0[c][:].indirect(offsets[:, hh * 32 : (hh + 1) * 32]),
-                    in1=y1[:],
-                    op=ALU.mult,
-                )
-                nc.sync.dma_start(out=out[c * P : (c + 1) * P, hh * HALF : (hh + 1) * HALF], in_=res[:])
+                last = c == NT - 1 and hh == HALVES - 1
+                piece = HALF // 2 if last else HALF
+                for j0 in range(0, HALF, piece):
+                    res = keep.tile([P, piece], F32, name=f"res_{c}_{hh}_{j0}")
+                    col = hh * HALF + j0
+                    nc.vector.tensor_tensor(
+                        out=res[:],
+                        in0=x0[c][:].indirect(offsets[:, col // 16 : (col + piece) // 16]),
+                        in1=y1[:, j0 : j0 + piece],
+                        op=ALU.mult,
+                    )
+                    nc.sync.dma_start(out=out[c * P : (c + 1) * P, col : col + piece], in_=res[:])

@@ -40,136 +40,138 @@ def tile_list_xcross_tanh_kernel(
         reuse = ctx.enter_context(tc.tile_pool(name="reuse", bufs=1))
 
         offsets = keep.tile([P, J // 16], U16, name="offsets")
-        tabs = reuse.tile([P, T], U8, name="tabs", offset=15872, align_bytes=64)
-        dn_raw = [keep.tile([P, PACK, R], F32, name=f"dn_raw{a}", tag=f"slot_raw{a}", align_bytes=64) for a in range(PASSES)]
+        tabs = reuse.tile([P, T], U8, name="tabs", offset=7680, align_bytes=64)
+        tabw = keep.tile([P, T], I32, name="tabw", tag="slot_tabw", align_bytes=64)
+        dn_raw = [keep.tile([P, PACK, R], F32, name="dn_raw0", tag="slot_raw0", align_bytes=64)]
         sm_t = keep.tile([P, PACK], F32, name="sm_t")
         b_rows = keep.tile([P, P], F32, name="b_rows")
         ident = keep.tile([P, P], F32, name="ident")
-        upw = keep.tile([P, 2 * N], U8, name="upw", align_bytes=64)
-        planes = keep.tile([P, PASSES * J + PASSES * N], U8, name="planes", align_bytes=64)
+        planes = keep.tile([P, PASSES * J + PASSES * N + N], U8, name="planes", align_bytes=64)
 
         nc.sync.dma_start(out=tabs[96:128, :].bitcast(I32), in_=tab_scales.rearrange("a q t -> (a q) t").bitcast(I32))
         nc.sync.dma_start(offsets[:], offs)
         nc.scalar.dma_start(out=sm_t[:], in_=sm.rearrange("(p t) -> p t", t=PACK))
-        for a in range(PASSES):
-            nc.sync.dma_start(out=dn_raw[a][:], in_=dn[512 * a : 512 * (a + 1), :].rearrange("(p i) r -> p i r", i=PACK))
+        nc.sync.dma_start(out=tabw[:], in_=tab_words[0].rearrange("p t i -> p (t i)").bitcast(I32))
+        nc.sync.dma_start(out=dn_raw[0][:], in_=dn[0:512, :].rearrange("(p i) r -> p i r", i=PACK))
 
-        nc.sync.dma_start(out=upw[:].bitcast(I32), in_=upw_words[0].bitcast(I32))
         nc.vector.memset(tabs[0:96, :].bitcast(I32), 0)
         nc.vector.memset(planes[:].bitcast(I32), 0)
         v_scales = [planes[:, a * J : (a + 1) * J] for a in range(PASSES)]
-        wbs = planes[:, PASSES * J :]
+        wbs = planes[:, PASSES * J : PASSES * J + PASSES * N]
+        ups = planes[:, PASSES * J + PASSES * N :]
+        nc.gpsimd.memset(b_rows[:], 0.0)
+        nc.gpsimd.dma_start(out=b_rows[0:NT, :], in_=b.rearrange("(c p) -> c p", p=P))
+        make_identity(nc, ident[:])
         for q in range(QUADS):
             nc.gpsimd.dma_start(
                 out=wbs[32 * q : 32 * q + 4, :].bitcast(I32).rearrange("r (a n) -> r a n", a=PASSES),
                 in_=wb_scales[:, 4 * q : 4 * q + 4, :].bitcast(I32).rearrange("a r n -> r a n"),
             )
-
-        nc.gpsimd.memset(b_rows[:], 0.0)
-        nc.gpsimd.dma_start(out=b_rows[0:NT, :], in_=b.rearrange("(c p) -> c p", p=P))
-        make_identity(nc, ident[:])
+        for q in range(QUADS):
+            nc.gpsimd.dma_start(
+                out=ups[32 * q : 32 * q + 4, :].bitcast(I32), in_=upw_scales[0, 4 * q : 4 * q + 4, :].bitcast(I32)
+            )
 
         picked_rows = keep.tile([P, J], U8, name="picked_rows", align_bytes=64)
         nc.vector.tensor_copy(out=picked_rows[:], in_=tabs[:].indirect(offsets[:]))
-        tabw = reuse.tile([P, T], I32, name="tabw", offset=0, align_bytes=64)
-        ups = reuse.tile([P, N], U8, name="ups", offset=16384, align_bytes=64)
-        wbw = reuse.tile([P, PASSES, N], I32, name="wbw", offset=16896, align_bytes=64)
-        nc.vector.memset(ups[:].bitcast(I32), 0)
+        dn_raw.append(reuse.tile([P, PACK, R], F32, name="dn_raw1", offset=0, align_bytes=64))
+        upw = reuse.tile([P, 2 * N], U8, name="upw", offset=8192, align_bytes=64)
+        wbw = reuse.tile([P, PASSES, N], I32, name="wbw", offset=9216, align_bytes=64)
         for a in range(PASSES):
-            for q in range(QUADS):
-                row = 96 + 16 * a + 4 * q
+            for r in range(4):
+                row = 96 + 16 * a + r
                 nc.sync.dma_start(
-                    out=v_scales[a][32 * q : 32 * q + 4, :].bitcast(I32), in_=picked_rows[row : row + 4, :].bitcast(I32)
+                    out=v_scales[a][r:128:32, :].bitcast(I32), in_=picked_rows[row : row + 13 : 4, :].bitcast(I32)
                 )
-                if (a, q) == (0, 1):
-                    nc.sync.dma_start(out=tabw[:], in_=tab_words[0].rearrange("p t i -> p (t i)").bitcast(I32))
-        nc.sync.dma_start(out=wbw[:], in_=wb_words.rearrange("a p n i -> p a (n i)").bitcast(I32))
+            if a == 0:
+                nc.sync.dma_start(out=dn_raw[1][:], in_=dn[512:1024, :].rearrange("(p i) r -> p i r", i=PACK))
+                nc.sync.dma_start(out=wbw[:], in_=wb_words.rearrange("a p n i -> p a (n i)").bitcast(I32))
+                nc.sync.dma_start(out=upw[:].bitcast(I32), in_=upw_words[0].bitcast(I32))
 
         b1 = keep.tile([P, NT], F32, name="b1")
         b_cols = y_psum.tile([P, HALF], F32, name="y")
         nc.tensor.transpose(b_cols[:, 0:P], b_rows[:], ident[:])
         nc.vector.tensor_scalar(out=b1[:], in0=b_cols[:, 0:NT], scalar1=1.0, scalar2=None, op0=ALU.add)
 
-        dn_codes, dn_scales = [], []
+        both = keep.tile([P, J], U32, name="both", tag="slot_both", align_bytes=64)
+        nc.vector.tensor_copy(out=both[:], in_=tabw[:].bitcast(U32).indirect(offsets[:]))
+        v_codes = keep.tile([P, PASSES * 2 * J], U8, name="v_codes", align_bytes=64)
+
+        dn_codes, dn_scales = {}, {}
         for a in range(PASSES):
-            dn_bf = keep.tile([P, R * PACK], BF16, name=f"dn_bf{a}", tag=f"slot_bf{a}", align_bytes=64)
-            nc.scalar.copy(
-                out=dn_bf[:].rearrange("p (t m i) -> p m i t", t=PACK, i=PACK),
-                in_=dn_raw[a][:].rearrange("p i (m t) -> p m i t", t=PACK),
-            )
-            codes = keep.tile([P, R], U32, name=f"dn_codes{a}", align_bytes=64)
-            scales = keep.tile([P, R], U8, name=f"dn_scales{a}", align_bytes=64)
-            nc.vector.quantize_mx(out=codes[:].bitcast(FP8X4), scales=scales[:], in_=dn_bf[:])
-            dn_codes.append(codes)
-            dn_scales.append(scales)
+            dn_bf = []
+            for g, copy in enumerate((nc.scalar.copy, nc.vector.tensor_copy)):
+                dn_bf.append(keep.tile([P, 2 * P * PACK], BF16, name=f"dn_bf{a}{g}", tag=f"slot_bf{a}{g}", align_bytes=64))
+                copy(
+                    out=dn_bf[g][:].rearrange("p (t m i) -> p m i t", t=2, i=PACK),
+                    in_=dn_raw[a][:].rearrange("p i (m t) -> p m i t", t=PACK)[:, :, :, 2 * g : 2 * g + 2],
+                )
+            if a == 0:
+                nc.vector.tensor_copy(
+                    out=v_codes[:].bitcast(U16).rearrange("p (a j) -> p a j", a=PASSES),
+                    in_=both[:].bitcast(U16).rearrange("p (j a) -> p a j", a=PASSES),
+                )
+            for g in range(2):
+                codes = keep.tile([P, 2 * P], U32, name=f"dn_codes{a}{g}", align_bytes=64)
+                scales = keep.tile([P, 2 * P], U8, name=f"dn_scales{a}{g}", align_bytes=64)
+                nc.vector.quantize_mx(out=codes[:].bitcast(FP8X4), scales=scales[:], in_=dn_bf[g][:])
+                for u in range(2):
+                    dn_codes[a, 2 * g + u] = codes[:, u * P : (u + 1) * P]
+                    dn_scales[a, 2 * g + u] = scales[:, u * P : (u + 1) * P]
 
         x0 = []
-        for c, slot in enumerate(("slot_raw0", "slot_bf0", "slot_raw1", "slot_bf1")):
+        for c, slot in enumerate(("slot_tabw", "slot_raw0", "slot_bf01", "slot_bf11")):
             x0.append(keep.tile([P, T], F32, name=f"x0_{c}", tag=slot, align_bytes=64))
             nc.sync.dma_start(out=x0[c][:], in_=x0T[c * P : (c + 1) * P, :])
-            if c == 0:
-                for q in range(QUADS):
-                    nc.sync.dma_start(
-                        out=ups[32 * q : 32 * q + 4, :].bitcast(I32), in_=upw_scales[0, 4 * q : 4 * q + 4, :].bitcast(I32)
-                    )
+        h_codes = keep.tile([P, J], U32, name="h_codes", align_bytes=64)
+        h_scales = keep.tile([P, J], U8, name="h_scales", align_bytes=64)
+        h_bf = []
 
-        v_codes = []
-        for hh in range(HALVES):
-            both = ring.tile([P, HALF], U32, name="both", align_bytes=64)
-            nc.vector.tensor_copy(
-                out=both[:], in_=tabw[:].bitcast(U32).indirect(offsets[:, hh * 32 : (hh + 1) * 32])
-            )
-            parted = keep.tile([P, PASSES * 2 * HALF], U8, name=f"v_codes{hh}", align_bytes=64)
-            nc.vector.tensor_copy(
-                out=parted[:].bitcast(U16).rearrange("p (a j) -> p a j", a=PASSES),
-                in_=both[:].bitcast(U16).rearrange("p (j a) -> p a j", a=PASSES),
-            )
-            v_codes.append(parted)
+        def quantise_h(pair):
+            cols = slice(pair * 2 * CH, (pair + 1) * 2 * CH)
+            nc.vector.quantize_mx(out=h_codes[:, cols].bitcast(FP8X4), scales=h_scales[:, cols], in_=h_bf[pair][:])
 
-        h_codes, h_scales = [], []
-        for hh in range(HALVES):
-            h_bf = ring.tile([P, HALF * PACK], BF16, name="h_bf", align_bytes=64)
-            for pair in range(2):
-                th = ring.tile([P, 2 * CH * PACK], F32, name="th")
-                for u in range(2):
-                    j0 = (2 * pair + u) * CH
-                    hs = hs_psum.tile([P, PACK, CH], F32, name="hs")
-                    for t in range(PACK):
-                        for a in range(PASSES):
-                            nc.tensor.matmul_mx(
-                                out=hs[:, t, :],
-                                lhsT=dn_codes[a][:, t * P : (t + 1) * P].bitcast(FP8X4),
-                                lhsT_scale=dn_scales[a][:, t * P : (t + 1) * P],
-                                rhs=v_codes[hh][:, 2 * (a * HALF + j0) : 2 * (a * HALF + j0 + CH)].bitcast(FP4X4),
-                                rhs_scale=v_scales[a][:, hh * HALF + j0 : hh * HALF + j0 + CH],
-                                start=(a == 0),
-                                stop=(a == PASSES - 1),
-                            )
-                    nc.scalar.activation(
-                        out=th[:, u * CH * PACK : (u + 1) * CH * PACK].rearrange("p (j t) -> p j t", t=PACK),
-                        in_=hs[:].rearrange("p t j -> p j t"),
-                        func=ACT.Tanh,
+        for bank in range(J // CH):
+            pair, u = divmod(bank, 2)
+            j0 = bank * CH
+            if u == 0:
+                h_bf.append(ring.tile([P, 2 * CH * PACK], BF16, name="h_bf", align_bytes=64))
+            hs = hs_psum.tile([P, PACK, CH], F32, name="hs")
+            for a in range(PASSES):
+                for t in range(PACK):
+                    nc.tensor.matmul_mx(
+                        out=hs[:, t, :],
+                        lhsT=dn_codes[a, t].bitcast(FP8X4),
+                        lhsT_scale=dn_scales[a, t],
+                        rhs=v_codes[:, 2 * (a * J + j0) : 2 * (a * J + j0 + CH)].bitcast(FP4X4),
+                        rhs_scale=v_scales[a][:, j0 : j0 + CH],
+                        start=(a == 0 and t == 0),
+                        stop=(a == PASSES - 1 and t == PACK - 1),
                     )
-                nc.vector.tensor_tensor(
-                    out=h_bf[:, pair * 2 * CH * PACK : (pair + 1) * 2 * CH * PACK].rearrange("p (j t) -> p j t", t=PACK),
-                    in0=th[:].rearrange("p (j t) -> p j t", t=PACK),
-                    in1=sm_t[:].unsqueeze(1).to_broadcast([P, 2 * CH, PACK]),
-                    op=ALU.mult,
-                )
-            h_codes.append(keep.tile([P, HALF], U32, name=f"h_codes{hh}", align_bytes=64))
-            h_scales.append(keep.tile([P, HALF], U8, name=f"h_scales{hh}", align_bytes=64))
-            nc.vector.quantize_mx(out=h_codes[hh][:].bitcast(FP8X4), scales=h_scales[hh][:], in_=h_bf[:])
+            th = ring.tile([P, CH, PACK], F32, name="th", bufs=4)
+            nc.scalar.activation(out=th[:], in_=hs[:].rearrange("p t j -> p j t"), func=ACT.Tanh)
+            nc.vector.tensor_tensor(
+                out=h_bf[pair][:, u * CH * PACK : (u + 1) * CH * PACK].rearrange("p (j t) -> p j t", t=PACK),
+                in0=th[:],
+                in1=sm_t[:].unsqueeze(1).to_broadcast([P, CH, PACK]),
+                op=ALU.mult,
+            )
+            if u == 0 and pair > 0:
+                quantise_h(pair - 1)
+        quantise_h(J // (2 * CH) - 1)
 
         for c in range(NT):
+            res = keep.tile([P, J], F32, name=f"res{c}")
             for hh in range(HALVES):
+                cols = slice(hh * HALF, (hh + 1) * HALF)
                 y = y_psum.tile([P, HALF], F32, name="y")
                 for a in range(PASSES):
                     nc.tensor.matmul_mx(
                         out=y[:],
                         lhsT=wbw[:, a, c * P : (c + 1) * P].bitcast(FP8X4),
                         lhsT_scale=wbs[:, a * N + c * P : a * N + (c + 1) * P],
-                        rhs=v_codes[hh][:, 2 * a * HALF : 2 * (a + 1) * HALF].bitcast(FP4X4),
-                        rhs_scale=v_scales[a][:, hh * HALF : (hh + 1) * HALF],
+                        rhs=v_codes[:, 2 * (a * J + hh * HALF) : 2 * (a * J + (hh + 1) * HALF)].bitcast(FP4X4),
+                        rhs_scale=v_scales[a][:, cols],
                         start=(a == 0),
                         stop=False,
                     )
@@ -177,22 +179,20 @@ def tile_list_xcross_tanh_kernel(
                     out=y[:],
                     lhsT=upw[:, 2 * c * P : 2 * (c + 1) * P].bitcast(FP4X4),
                     lhsT_scale=ups[:, c * P : (c + 1) * P],
-                    rhs=h_codes[hh][:].bitcast(FP8X4),
-                    rhs_scale=h_scales[hh][:],
+                    rhs=h_codes[:, cols].bitcast(FP8X4),
+                    rhs_scale=h_scales[:, cols],
                     start=False,
                     stop=True,
                 )
                 y1 = ring.tile([P, HALF], F32, name="y1", bufs=3)
                 nc.scalar.activation(out=y1[:], in_=y[:], func=ACT.Identity, bias=b1[:, c : c + 1])
-                last = c == NT - 1 and hh == HALVES - 1
-                piece = HALF // 2 if last else HALF
-                for j0 in range(0, HALF, piece):
-                    res = keep.tile([P, piece], F32, name=f"res_{c}_{hh}_{j0}")
-                    col = hh * HALF + j0
-                    nc.vector.tensor_tensor(
-                        out=res[:],
-                        in0=x0[c][:].indirect(offsets[:, col // 16 : (col + piece) // 16]),
-                        in1=y1[:, j0 : j0 + piece],
-                        op=ALU.mult,
-                    )
-                    nc.sync.dma_start(out=out[c * P : (c + 1) * P, col : col + piece], in_=res[:])
+                nc.vector.tensor_tensor(
+                    out=res[:, cols],
+                    in0=x0[c][:].indirect(offsets[:, hh * HALF // 16 : (hh + 1) * HALF // 16]),
+                    in1=y1[:],
+                    op=ALU.mult,
+                )
+                if c == NT - 1:
+                    nc.sync.dma_start(out=out[c * P : (c + 1) * P, cols], in_=res[:, cols])
+            if c < NT - 1:
+                nc.sync.dma_start(out=out[c * P : (c + 1) * P, :], in_=res[:])

@@ -46,9 +46,9 @@ def tile_list_xcross_tanh_kernel(
         sm_t = keep.tile([P, PACK], F32, name="sm_t")
         b_rows = keep.tile([P, P], F32, name="b_rows")
         ident = keep.tile([P, P], F32, name="ident")
-        planes = keep.tile([P, PASSES * J + PASSES * N + N], U8, name="planes", align_bytes=64)
+        planes = keep.tile([P, PASSES * J], U8, name="planes", align_bytes=64)
 
-        nc.sync.dma_start(out=tabs[96:128, :].bitcast(I32), in_=tab_scales.rearrange("a q t -> (a q) t").bitcast(I32))
+        nc.sync.dma_start(out=tabs[96:128, :].bitcast(I32), in_=tab_scales.bitcast(I32).rearrange("a q t -> q a t"))
         nc.sync.dma_start(offsets[:], offs)
         nc.scalar.dma_start(out=sm_t[:], in_=sm.rearrange("(p t) -> p t", t=PACK))
         nc.sync.dma_start(out=tabw[:], in_=tab_words[0].rearrange("p t i -> p (t i)").bitcast(I32))
@@ -57,36 +57,30 @@ def tile_list_xcross_tanh_kernel(
         nc.vector.memset(tabs[0:96, :].bitcast(I32), 0)
         nc.vector.memset(planes[:].bitcast(I32), 0)
         v_scales = [planes[:, a * J : (a + 1) * J] for a in range(PASSES)]
-        wbs = planes[:, PASSES * J : PASSES * J + PASSES * N]
-        ups = planes[:, PASSES * J + PASSES * N :]
         nc.gpsimd.memset(b_rows[:], 0.0)
-        nc.gpsimd.dma_start(out=b_rows[0:NT, :], in_=b.rearrange("(c p) -> c p", p=P))
+        nc.scalar.dma_start(out=b_rows[0:NT, :], in_=b.rearrange("(c p) -> c p", p=P))
         make_identity(nc, ident[:])
-        for q in range(QUADS):
-            nc.gpsimd.dma_start(
-                out=wbs[32 * q : 32 * q + 4, :].bitcast(I32).rearrange("r (a n) -> r a n", a=PASSES),
-                in_=wb_scales[:, 4 * q : 4 * q + 4, :].bitcast(I32).rearrange("a r n -> r a n"),
-            )
-        for q in range(QUADS):
-            nc.gpsimd.dma_start(
-                out=ups[32 * q : 32 * q + 4, :].bitcast(I32), in_=upw_scales[0, 4 * q : 4 * q + 4, :].bitcast(I32)
-            )
 
         picked_rows = keep.tile([P, J], U8, name="picked_rows", align_bytes=64)
         nc.vector.tensor_copy(out=picked_rows[:], in_=tabs[:].indirect(offsets[:]))
         dn_raw.append(reuse.tile([P, PACK, R], F32, name="dn_raw1", offset=0, align_bytes=64))
         upw = reuse.tile([P, 2 * N], U8, name="upw", offset=8192, align_bytes=64)
-        wbw = reuse.tile([P, PASSES, N], I32, name="wbw", offset=9216, align_bytes=64)
-        for a in range(PASSES):
-            for r in range(4):
-                row = 96 + 16 * a + r
-                nc.sync.dma_start(
-                    out=v_scales[a][r:128:32, :].bitcast(I32), in_=picked_rows[row : row + 13 : 4, :].bitcast(I32)
-                )
-            if a == 0:
-                nc.sync.dma_start(out=dn_raw[1][:], in_=dn[512:1024, :].rearrange("(p i) r -> p i r", i=PACK))
-                nc.sync.dma_start(out=wbw[:], in_=wb_words.rearrange("a p n i -> p a (n i)").bitcast(I32))
-                nc.sync.dma_start(out=upw[:].bitcast(I32), in_=upw_words[0].bitcast(I32))
+        wbs = reuse.tile([P, PASSES * N], U8, name="wbs", offset=9216, align_bytes=64)
+        wbw = reuse.tile([P, PASSES, N], I32, name="wbw", offset=10240, align_bytes=64)
+        nc.vector.memset(wbs[:].bitcast(I32), 0)
+        for q in range(QUADS):
+            nc.sync.dma_start(
+                out=planes[32 * q : 32 * q + 4, 0 : PASSES * J].bitcast(I32),
+                in_=picked_rows[96 + 8 * q : 96 + 8 * q + 8, :].bitcast(I32),
+            )
+        nc.sync.dma_start(out=dn_raw[1][:], in_=dn[512:1024, :].rearrange("(p i) r -> p i r", i=PACK))
+        nc.sync.dma_start(out=wbw[:], in_=wb_words.rearrange("a p n i -> p a (n i)").bitcast(I32))
+        for q in range(QUADS):
+            nc.sync.dma_start(
+                out=wbs[32 * q : 32 * q + 4, :].bitcast(I32).rearrange("r (a n) -> r a n", a=PASSES),
+                in_=wb_scales[:, 4 * q : 4 * q + 4, :].bitcast(I32).rearrange("a r n -> r a n"),
+            )
+        nc.sync.dma_start(out=upw[:].bitcast(I32), in_=upw_words[0].bitcast(I32))
 
         b1 = keep.tile([P, NT], F32, name="b1")
         b_cols = y_psum.tile([P, HALF], F32, name="y")
@@ -123,6 +117,13 @@ def tile_list_xcross_tanh_kernel(
         for c, slot in enumerate(("slot_tabw", "slot_raw0", "slot_bf01", "slot_bf11")):
             x0.append(keep.tile([P, T], F32, name=f"x0_{c}", tag=slot, align_bytes=64))
             nc.sync.dma_start(out=x0[c][:], in_=x0T[c * P : (c + 1) * P, :])
+            if c == 0:
+                ups = keep.tile([P, N], U8, name="ups", tag="slot_both", align_bytes=64)
+                nc.vector.memset(ups[:].bitcast(I32), 0)
+                for q in range(QUADS):
+                    nc.sync.dma_start(
+                        out=ups[32 * q : 32 * q + 4, :].bitcast(I32), in_=upw_scales[0, 4 * q : 4 * q + 4, :].bitcast(I32)
+                    )
         h_codes = keep.tile([P, J], U32, name="h_codes", align_bytes=64)
         h_scales = keep.tile([P, J], U8, name="h_scales", align_bytes=64)
         h_bf = []

@@ -25,6 +25,9 @@ HALVES = J // HALF
 CH = 128
 NT = N // P
 QUADS = 4
+SCALAR_M = 40
+EARLY_BANKS = 3
+Y_BANKS = 3
 
 
 def tile_list_xcross_tanh_kernel(
@@ -34,9 +37,9 @@ def tile_list_xcross_tanh_kernel(
     with ExitStack() as ctx:
         keep = ctx.enter_context(tc.tile_pool(name="keep", bufs=1))
         ring = ctx.enter_context(tc.tile_pool(name="ring", bufs=2))
-        hs_psum = ctx.enter_context(tc.psum_pool(name="hs_psum", bufs=4))
-        y_psum = ctx.enter_context(tc.psum_pool(name="y_psum", bufs=4))
+        psum = ctx.enter_context(tc.psum_pool(name="psum", bufs=1))
 
+        late = ctx.enter_context(tc.tile_pool(name="late", bufs=1))
         reuse = ctx.enter_context(tc.tile_pool(name="reuse", bufs=1))
 
         offsets = keep.tile([P, J // 16], U16, name="offsets")
@@ -68,132 +71,181 @@ def tile_list_xcross_tanh_kernel(
         wbs = reuse.tile([P, PASSES * N], U8, name="wbs", offset=9216, align_bytes=64)
         wbw = reuse.tile([P, PASSES, N], I32, name="wbw", offset=10240, align_bytes=64)
         nc.vector.memset(wbs[:].bitcast(I32), 0)
-        for q in range(QUADS):
+        for q in (0, 2, 1, 3):
             nc.sync.dma_start(
                 out=planes[32 * q : 32 * q + 4, 0 : PASSES * J].bitcast(I32),
                 in_=picked_rows[96 + 8 * q : 96 + 8 * q + 8, :].bitcast(I32),
             )
         nc.sync.dma_start(out=dn_raw[1][:], in_=dn[512:1024, :].rearrange("(p i) r -> p i r", i=PACK))
         nc.sync.dma_start(out=wbw[:], in_=wb_words.rearrange("a p n i -> p a (n i)").bitcast(I32))
-        for q in range(QUADS):
+        for r in range(4):
             nc.sync.dma_start(
-                out=wbs[32 * q : 32 * q + 4, :].bitcast(I32).rearrange("r (a n) -> r a n", a=PASSES),
-                in_=wb_scales[:, 4 * q : 4 * q + 4, :].bitcast(I32).rearrange("a r n -> r a n"),
+                out=wbs[r:128:32, :].bitcast(I32).rearrange("q (a n) -> q a n", a=PASSES),
+                in_=wb_scales[:, r:16:4, :].bitcast(I32).rearrange("a q n -> q a n"),
             )
         nc.sync.dma_start(out=upw[:].bitcast(I32), in_=upw_words[0].bitcast(I32))
 
-        b1 = keep.tile([P, NT], F32, name="b1")
-        b_cols = y_psum.tile([P, HALF], F32, name="y")
+        b_cols = psum.tile([P, HALF], F32, name="b_cols", tag=f"bank{EARLY_BANKS}")
         nc.tensor.transpose(b_cols[:, 0:P], b_rows[:], ident[:])
-        nc.vector.tensor_scalar(out=b1[:], in0=b_cols[:, 0:NT], scalar1=1.0, scalar2=None, op0=ALU.add)
 
-        both = keep.tile([P, J], U32, name="both", tag="slot_both", align_bytes=64)
-        nc.vector.tensor_copy(out=both[:], in_=tabw[:].bitcast(U32).indirect(offsets[:]))
-        v_codes = keep.tile([P, PASSES * 2 * J], U8, name="v_codes", align_bytes=64)
+        both, v_codes = [], []
+
+        def part_words(hh, codes):
+            v_codes.append(codes)
+            nc.vector.tensor_copy(
+                out=v_codes[hh][:].bitcast(U16).rearrange("p (a j) -> p a j", a=PASSES),
+                in_=both[hh][:].bitcast(U16).rearrange("p (j a) -> p a j", a=PASSES),
+            )
+
+        for hh in range(HALVES):
+            both.append(keep.tile([P, HALF], U32, name=f"both{hh}", tag=f"slot_both{hh}", align_bytes=64))
+            nc.vector.tensor_copy(
+                out=both[hh][:], in_=tabw[:].bitcast(U32).indirect(offsets[:, hh * HALF // 16 : (hh + 1) * HALF // 16])
+            )
+            if hh == 0:
+                part_words(0, keep.tile([P, PASSES * 2 * HALF], U8, name="v_codes0", align_bytes=64))
+        x0 = []
+
+        def load_x0(pool, **place):
+            c = len(x0)
+            x0.append(pool.tile([P, T], F32, name=f"x0_{c}", align_bytes=64, **place))
+            nc.sync.dma_start(out=x0[c][:], in_=x0T[c * P : (c + 1) * P, :])
+
+        load_x0(keep, tag="slot_tabw")
 
         dn_codes, dn_scales = {}, {}
-        for a in range(PASSES):
-            dn_bf = []
-            for g, copy in enumerate((nc.scalar.copy, nc.vector.tensor_copy)):
-                dn_bf.append(keep.tile([P, 2 * P * PACK], BF16, name=f"dn_bf{a}{g}", tag=f"slot_bf{a}{g}", align_bytes=64))
-                copy(
-                    out=dn_bf[g][:].rearrange("p (t m i) -> p m i t", t=2, i=PACK),
-                    in_=dn_raw[a][:].rearrange("p i (m t) -> p m i t", t=PACK)[:, :, :, 2 * g : 2 * g + 2],
-                )
-            if a == 0:
-                nc.vector.tensor_copy(
-                    out=v_codes[:].bitcast(U16).rearrange("p (a j) -> p a j", a=PASSES),
-                    in_=both[:].bitcast(U16).rearrange("p (j a) -> p a j", a=PASSES),
-                )
-            for g in range(2):
-                codes = keep.tile([P, 2 * P], U32, name=f"dn_codes{a}{g}", align_bytes=64)
-                scales = keep.tile([P, 2 * P], U8, name=f"dn_scales{a}{g}", align_bytes=64)
-                nc.vector.quantize_mx(out=codes[:].bitcast(FP8X4), scales=scales[:], in_=dn_bf[g][:])
-                for u in range(2):
-                    dn_codes[a, 2 * g + u] = codes[:, u * P : (u + 1) * P]
-                    dn_scales[a, 2 * g + u] = scales[:, u * P : (u + 1) * P]
 
-        x0 = []
-        for c, slot in enumerate(("slot_tabw", "slot_raw0", "slot_bf01", "slot_bf11")):
-            x0.append(keep.tile([P, T], F32, name=f"x0_{c}", tag=slot, align_bytes=64))
-            nc.sync.dma_start(out=x0[c][:], in_=x0T[c * P : (c + 1) * P, :])
-            if c == 0:
-                ups = keep.tile([P, N], U8, name="ups", tag="slot_both", align_bytes=64)
-                nc.vector.memset(ups[:].bitcast(I32), 0)
-                for q in range(QUADS):
-                    nc.sync.dma_start(
-                        out=ups[32 * q : 32 * q + 4, :].bitcast(I32), in_=upw_scales[0, 4 * q : 4 * q + 4, :].bitcast(I32)
-                    )
-        h_codes = keep.tile([P, J], U32, name="h_codes", align_bytes=64)
-        h_scales = keep.tile([P, J], U8, name="h_scales", align_bytes=64)
+        def quantise_dn(a, t0, dn_bf):
+            width = dn_bf.shape[1] // PACK
+            codes = keep.tile([P, width], U32, name=f"dn_codes{a}{t0}", align_bytes=64)
+            scales = keep.tile([P, width], U8, name=f"dn_scales{a}{t0}", align_bytes=64)
+            nc.vector.quantize_mx(out=codes[:].bitcast(FP8X4), scales=scales[:], in_=dn_bf[:])
+            for u in range(width // P):
+                dn_codes[a, t0 + u] = codes[:, u * P : (u + 1) * P]
+                dn_scales[a, t0 + u] = scales[:, u * P : (u + 1) * P]
+
+        dn_bf0 = []
+        for g, copy in enumerate((nc.scalar.copy, nc.vector.tensor_copy)):
+            dn_bf0.append(keep.tile([P, 2 * P * PACK], BF16, name=f"dn_bf0{g}", tag=f"slot_bf0{g}", align_bytes=64))
+            copy(
+                out=dn_bf0[g][:].rearrange("p (t m i) -> p m i t", t=2, i=PACK),
+                in_=dn_raw[0][:].rearrange("p i (m t) -> p m i t", t=PACK)[:, :, :, 2 * g : 2 * g + 2],
+            )
+        ups = keep.tile([P, N], U8, name="ups", tag="slot_raw0", align_bytes=64)
+        nc.vector.memset(ups[:].bitcast(I32), 0)
+        for r in range(4):
+            nc.sync.dma_start(out=ups[r:128:32, :].bitcast(I32), in_=upw_scales[0, r:16:4, :].bitcast(I32))
+        for g in (1, 0):
+            quantise_dn(0, 2 * g, dn_bf0[g])
+
+        dn_bf1 = late.tile([P, PACK * P * PACK], BF16, name="dn_bf1", offset=0, align_bytes=64)
+        for copy, ms in ((nc.scalar.copy, slice(0, SCALAR_M)), (nc.vector.tensor_copy, slice(SCALAR_M, P))):
+            copy(
+                out=dn_bf1[:].rearrange("p (t m i) -> p m i t", t=PACK, i=PACK)[:, ms, :, :],
+                in_=dn_raw[1][:].rearrange("p i (m t) -> p m i t", t=PACK)[:, ms, :, :],
+            )
+        quantise_dn(1, 0, dn_bf1)
+        b1 = late.tile([P, NT], F32, name="b1", offset=0, align_bytes=64)
+        nc.vector.tensor_scalar(out=b1[:], in0=b_cols[:, 0:NT], scalar1=1.0, scalar2=None, op0=ALU.add)
+        part_words(1, late.tile([P, PASSES * 2 * HALF], U8, name="v_codes1", offset=64, align_bytes=64))
+        load_x0(keep, tag="slot_bf00")
+        load_x0(late, offset=64 + PASSES * 2 * HALF)
+        load_x0(keep, tag="slot_both1")
+        h_codes = [keep.tile([P, HALF], U32, name=f"h_codes{hh}", align_bytes=64) for hh in range(HALVES)]
+        h_scales = [keep.tile([P, HALF], U8, name=f"h_scales{hh}", align_bytes=64) for hh in range(HALVES)]
         h_bf = []
 
         def quantise_h(pair):
-            cols = slice(pair * 2 * CH, (pair + 1) * 2 * CH)
-            nc.vector.quantize_mx(out=h_codes[:, cols].bitcast(FP8X4), scales=h_scales[:, cols], in_=h_bf[pair][:])
+            hh, part = divmod(pair, 2)
+            cols = slice(part * 2 * CH, (part + 1) * 2 * CH)
+            nc.vector.quantize_mx(
+                out=h_codes[hh][:, cols].bitcast(FP8X4), scales=h_scales[hh][:, cols], in_=h_bf[pair][:]
+            )
 
         for bank in range(J // CH):
             pair, u = divmod(bank, 2)
             j0 = bank * CH
             if u == 0:
                 h_bf.append(ring.tile([P, 2 * CH * PACK], BF16, name="h_bf", align_bytes=64))
-            hs = hs_psum.tile([P, PACK, CH], F32, name="hs")
+                th = ring.tile([P, 2 * CH, PACK], F32, name="th", bufs=3)
+            hs = psum.tile([P, PACK, CH], F32, name="hs", tag=f"bank{bank}")
             for a in range(PASSES):
-                for t in range(PACK):
+                for k, t in enumerate((2, 3, 0, 1)):
                     nc.tensor.matmul_mx(
                         out=hs[:, t, :],
                         lhsT=dn_codes[a, t].bitcast(FP8X4),
                         lhsT_scale=dn_scales[a, t],
-                        rhs=v_codes[:, 2 * (a * J + j0) : 2 * (a * J + j0 + CH)].bitcast(FP4X4),
+                        rhs=v_codes[j0 // HALF][:, 2 * (a * HALF + j0 % HALF) : 2 * (a * HALF + j0 % HALF + CH)].bitcast(FP4X4),
                         rhs_scale=v_scales[a][:, j0 : j0 + CH],
-                        start=(a == 0 and t == 0),
-                        stop=(a == PASSES - 1 and t == PACK - 1),
+                        start=(a == 0 and k == 0),
+                        stop=(a == PASSES - 1 and k == PACK - 1),
                     )
-            th = ring.tile([P, CH, PACK], F32, name="th", bufs=4)
-            nc.scalar.activation(out=th[:], in_=hs[:].rearrange("p t j -> p j t"), func=ACT.Tanh)
-            nc.vector.tensor_tensor(
-                out=h_bf[pair][:, u * CH * PACK : (u + 1) * CH * PACK].rearrange("p (j t) -> p j t", t=PACK),
-                in0=th[:],
-                in1=sm_t[:].unsqueeze(1).to_broadcast([P, CH, PACK]),
-                op=ALU.mult,
-            )
-            if u == 0 and pair > 0:
-                quantise_h(pair - 1)
-        quantise_h(J // (2 * CH) - 1)
-
-        for c in range(NT):
-            res = keep.tile([P, J], F32, name=f"res{c}")
-            for hh in range(HALVES):
-                cols = slice(hh * HALF, (hh + 1) * HALF)
-                y = y_psum.tile([P, HALF], F32, name="y")
-                for a in range(PASSES):
-                    nc.tensor.matmul_mx(
-                        out=y[:],
-                        lhsT=wbw[:, a, c * P : (c + 1) * P].bitcast(FP8X4),
-                        lhsT_scale=wbs[:, a * N + c * P : a * N + (c + 1) * P],
-                        rhs=v_codes[:, 2 * (a * J + hh * HALF) : 2 * (a * J + (hh + 1) * HALF)].bitcast(FP4X4),
-                        rhs_scale=v_scales[a][:, cols],
-                        start=(a == 0),
-                        stop=False,
-                    )
-                nc.tensor.matmul_mx(
-                    out=y[:],
-                    lhsT=upw[:, 2 * c * P : 2 * (c + 1) * P].bitcast(FP4X4),
-                    lhsT_scale=ups[:, c * P : (c + 1) * P],
-                    rhs=h_codes[:, cols].bitcast(FP8X4),
-                    rhs_scale=h_scales[:, cols],
-                    start=False,
-                    stop=True,
-                )
-                y1 = ring.tile([P, HALF], F32, name="y1", bufs=3)
-                nc.scalar.activation(out=y1[:], in_=y[:], func=ACT.Identity, bias=b1[:, c : c + 1])
+            nc.scalar.activation(out=th[:, u * CH : (u + 1) * CH, :], in_=hs[:].rearrange("p t j -> p j t"), func=ACT.Tanh)
+            if pair == 0 or u == 1:
+                js = slice(u * CH, (u + 1) * CH) if pair == 0 else slice(0, 2 * CH)
                 nc.vector.tensor_tensor(
-                    out=res[:, cols],
-                    in0=x0[c][:].indirect(offsets[:, hh * HALF // 16 : (hh + 1) * HALF // 16]),
-                    in1=y1[:],
+                    out=h_bf[pair][:].rearrange("p (j t) -> p j t", t=PACK)[:, js, :],
+                    in0=th[:, js, :],
+                    in1=sm_t[:].unsqueeze(1).to_broadcast([P, js.stop - js.start, PACK]),
                     op=ALU.mult,
                 )
-                if c == NT - 1:
-                    nc.sync.dma_start(out=out[c * P : (c + 1) * P, cols], in_=res[:, cols])
-            if c < NT - 1:
-                nc.sync.dma_start(out=out[c * P : (c + 1) * P, :], in_=res[:])
+                if pair > 0:
+                    quantise_h(pair - 1)
+        quantise_h(J // (2 * CH) - 1)
+
+        res = [keep.tile([P, J], F32, name=f"res{c}") for c in range(NT)]
+        y1 = [keep.tile([P, J], F32, name=f"y1_{c}") for c in range(NT)]
+        banks_used = []
+
+        def make_y1(c, hh):
+            cols = slice(hh * HALF, (hh + 1) * HALF)
+            y = psum.tile([P, HALF], F32, name="y", tag=f"bank{len(banks_used) % Y_BANKS}")
+            banks_used.append(y)
+            for a in range(PASSES):
+                nc.tensor.matmul_mx(
+                    out=y[:],
+                    lhsT=wbw[:, a, c * P : (c + 1) * P].bitcast(FP8X4),
+                    lhsT_scale=wbs[:, a * N + c * P : a * N + (c + 1) * P],
+                    rhs=v_codes[hh][:, 2 * a * HALF : 2 * (a + 1) * HALF].bitcast(FP4X4),
+                    rhs_scale=v_scales[a][:, cols],
+                    start=(a == 0),
+                    stop=False,
+                )
+            nc.tensor.matmul_mx(
+                out=y[:],
+                lhsT=upw[:, 2 * c * P : 2 * (c + 1) * P].bitcast(FP4X4),
+                lhsT_scale=ups[:, c * P : (c + 1) * P],
+                rhs=h_codes[hh][:].bitcast(FP8X4),
+                rhs_scale=h_scales[hh][:],
+                start=False,
+                stop=True,
+            )
+            nc.scalar.activation(out=y1[c][:, cols], in_=y[:], func=ACT.Identity, bias=b1[:, c : c + 1])
+
+        def cross(c, cols):
+            nc.vector.tensor_tensor(
+                out=res[c][:, cols],
+                in0=x0[c][:].indirect(offsets[:, cols.start // 16 : cols.stop // 16]),
+                in1=y1[c][:, cols],
+                op=ALU.mult,
+            )
+
+        def store(c, cols):
+            nc.sync.dma_start(out=out[c * P : (c + 1) * P, cols], in_=res[c][:, cols])
+
+        halves = [slice(hh * HALF, (hh + 1) * HALF) for hh in range(HALVES)]
+        whole = slice(0, J)
+        for hh in range(HALVES):
+            for c in (0, 1):
+                make_y1(c, hh)
+                cross(c, halves[hh])
+                if hh == HALVES - 1:
+                    store(c, whole)
+        for hh in range(HALVES):
+            make_y1(2, hh)
+        cross(2, whole)
+        store(2, whole)
+        for hh in range(HALVES):
+            make_y1(3, hh)
+            cross(3, halves[hh])
+            store(3, halves[hh])

@@ -28,6 +28,7 @@ QUADS = 4
 SCALAR_M = 40
 EARLY_BANKS = 3
 Y_BANKS = 3
+LAST_SPLIT = 704
 
 
 def tile_list_xcross_tanh_kernel(
@@ -44,7 +45,7 @@ def tile_list_xcross_tanh_kernel(
 
         offsets = keep.tile([P, J // 16], U16, name="offsets")
         tabs = reuse.tile([P, T], U8, name="tabs", offset=7680, align_bytes=64)
-        tabw = keep.tile([P, T], I32, name="tabw", tag="slot_tabw", align_bytes=64)
+        tabw = keep.tile([P, T], I32, name="tabw", align_bytes=64)
         dn_raw = [keep.tile([P, PACK, R], F32, name="dn_raw0", tag="slot_raw0", align_bytes=64)]
         sm_t = keep.tile([P, PACK], F32, name="sm_t")
         b_rows = keep.tile([P, P], F32, name="b_rows")
@@ -64,7 +65,7 @@ def tile_list_xcross_tanh_kernel(
         nc.scalar.dma_start(out=b_rows[0:NT, :], in_=b.rearrange("(c p) -> c p", p=P))
         make_identity(nc, ident[:])
 
-        picked_rows = keep.tile([P, J], U8, name="picked_rows", align_bytes=64)
+        picked_rows = keep.tile([P, J], U8, name="picked_rows", tag="slot_rows", align_bytes=64)
         nc.vector.tensor_copy(out=picked_rows[:], in_=tabs[:].indirect(offsets[:]))
         dn_raw.append(reuse.tile([P, PACK, R], F32, name="dn_raw1", offset=0, align_bytes=64))
         upw = reuse.tile([P, 2 * N], U8, name="upw", offset=8192, align_bytes=64)
@@ -111,7 +112,7 @@ def tile_list_xcross_tanh_kernel(
             x0.append(pool.tile([P, T], F32, name=f"x0_{c}", align_bytes=64, **place))
             nc.sync.dma_start(out=x0[c][:], in_=x0T[c * P : (c + 1) * P, :])
 
-        load_x0(keep, tag="slot_tabw")
+        load_x0(keep, tag="slot_rows")
 
         dn_codes, dn_scales = {}, {}
 
@@ -247,5 +248,6 @@ def tile_list_xcross_tanh_kernel(
         store(2, whole)
         for hh in range(HALVES):
             make_y1(3, hh)
-            cross(3, halves[hh])
-            store(3, halves[hh])
+        for cols in (slice(0, LAST_SPLIT), slice(LAST_SPLIT, J)):
+            cross(3, cols)
+            store(3, cols)

@@ -44,47 +44,60 @@ def tile_list_xcross_tanh_kernel(
         reuse = ctx.enter_context(tc.tile_pool(name="reuse", bufs=1))
 
         offsets = keep.tile([P, J // 16], U16, name="offsets")
-        tabs = reuse.tile([P, T], U8, name="tabs", offset=7680, align_bytes=64)
+        tabs = reuse.tile([P, 6784], U8, name="tabs", offset=8128, align_bytes=64)
         tabw = keep.tile([P, T], I32, name="tabw", align_bytes=64)
-        dn_raw = [keep.tile([P, PACK, R], F32, name="dn_raw0", tag="slot_raw0", align_bytes=64)]
+        dn_raw = [keep.tile([P, PACK, R], F32, name="dn_raw0", align_bytes=64)]
         sm_t = keep.tile([P, PACK], F32, name="sm_t")
         b_rows = keep.tile([P, P], F32, name="b_rows")
         ident = keep.tile([P, P], F32, name="ident")
         planes = keep.tile([P, PASSES * J], U8, name="planes", align_bytes=64)
 
-        nc.sync.dma_start(out=tabs[96:128, :].bitcast(I32), in_=tab_scales.bitcast(I32).rearrange("a q t -> q a t"))
+        nc.sync.dma_start(out=tabs[96:128, 0:T].bitcast(I32), in_=tab_scales.bitcast(I32).rearrange("a q t -> q a t"))
         nc.sync.dma_start(offsets[:], offs)
         nc.scalar.dma_start(out=sm_t[:], in_=sm.rearrange("(p t) -> p t", t=PACK))
         nc.sync.dma_start(out=tabw[:], in_=tab_words[0].rearrange("p t i -> p (t i)").bitcast(I32))
         nc.sync.dma_start(out=dn_raw[0][:], in_=dn[0:512, :].rearrange("(p i) r -> p i r", i=PACK))
 
-        nc.vector.memset(tabs[0:96, :].bitcast(I32), 0)
+        nc.vector.memset(tabs[0:96, 0:T].bitcast(I32), 0)
         nc.vector.memset(planes[:].bitcast(I32), 0)
         v_scales = [planes[:, a * J : (a + 1) * J] for a in range(PASSES)]
         nc.gpsimd.memset(b_rows[:], 0.0)
         nc.scalar.dma_start(out=b_rows[0:NT, :], in_=b.rearrange("(c p) -> c p", p=P))
         make_identity(nc, ident[:])
 
-        picked_rows = keep.tile([P, J], U8, name="picked_rows", tag="slot_rows", align_bytes=64)
-        nc.vector.tensor_copy(out=picked_rows[:], in_=tabs[:].indirect(offsets[:]))
+        picked_rows = keep.tile([P, J], U8, name="picked_rows", align_bytes=64)
+        nc.vector.tensor_copy(out=picked_rows[:], in_=tabs[:, 0:T].indirect(offsets[:]))
         dn_raw.append(reuse.tile([P, PACK, R], F32, name="dn_raw1", offset=0, align_bytes=64))
         upw = reuse.tile([P, 2 * N], U8, name="upw", offset=8192, align_bytes=64)
-        wbs = reuse.tile([P, PASSES * N], U8, name="wbs", offset=9216, align_bytes=64)
-        wbw = reuse.tile([P, PASSES, N], I32, name="wbw", offset=10240, align_bytes=64)
-        nc.vector.memset(wbs[:].bitcast(I32), 0)
+        wscales = reuse.tile([P, (PASSES + 1) * N], U8, name="wscales", offset=9216, align_bytes=64)
+        wbw = reuse.tile([P, PASSES, N], I32, name="wbw", offset=10752, align_bytes=64)
+        x0 = [reuse.tile([P, T], F32, name="x0_0", offset=14848, align_bytes=64)]
+        wbs, ups = wscales[:, 0 : PASSES * N], wscales[:, PASSES * N :]
+        nc.vector.memset(wscales[:].bitcast(I32), 0)
         for q in (0, 2, 1, 3):
             nc.sync.dma_start(
                 out=planes[32 * q : 32 * q + 4, 0 : PASSES * J].bitcast(I32),
                 in_=picked_rows[96 + 8 * q : 96 + 8 * q + 8, :].bitcast(I32),
             )
+
+        def load_up_scales(r):
+            nc.sync.dma_start(
+                out=wscales[r:128:32, PASSES * N :].bitcast(I32), in_=upw_scales[0, r:16:4, :].bitcast(I32)
+            )
+
         nc.sync.dma_start(out=dn_raw[1][:], in_=dn[512:1024, :].rearrange("(p i) r -> p i r", i=PACK))
         nc.sync.dma_start(out=wbw[:], in_=wb_words.rearrange("a p n i -> p a (n i)").bitcast(I32))
+        nc.sync.dma_start(out=upw[:].bitcast(I32), in_=upw_words[0].bitcast(I32))
+        for r in (0, 1):
+            load_up_scales(r)
+        nc.sync.dma_start(out=x0[0][:], in_=x0T[0:P, :])
         for r in range(4):
             nc.sync.dma_start(
-                out=wbs[r:128:32, :].bitcast(I32).rearrange("q (a n) -> q a n", a=PASSES),
+                out=wscales[r:128:32, 0 : PASSES * N].bitcast(I32).rearrange("q (a n) -> q a n", a=PASSES),
                 in_=wb_scales[:, r:16:4, :].bitcast(I32).rearrange("a q n -> q a n"),
             )
-        nc.sync.dma_start(out=upw[:].bitcast(I32), in_=upw_words[0].bitcast(I32))
+        for r in (2, 3):
+            load_up_scales(r)
 
         b_cols = psum.tile([P, HALF], F32, name="b_cols", tag=f"bank{EARLY_BANKS}")
         nc.tensor.transpose(b_cols[:, 0:P], b_rows[:], ident[:])
@@ -105,14 +118,12 @@ def tile_list_xcross_tanh_kernel(
             )
             if hh == 0:
                 part_words(0, keep.tile([P, PASSES * 2 * HALF], U8, name="v_codes0", align_bytes=64))
-        x0 = []
 
         def load_x0(pool, **place):
             c = len(x0)
             x0.append(pool.tile([P, T], F32, name=f"x0_{c}", align_bytes=64, **place))
             nc.sync.dma_start(out=x0[c][:], in_=x0T[c * P : (c + 1) * P, :])
 
-        load_x0(keep, tag="slot_rows")
 
         dn_codes, dn_scales = {}, {}
 
@@ -132,10 +143,6 @@ def tile_list_xcross_tanh_kernel(
                 out=dn_bf0[g][:].rearrange("p (t m i) -> p m i t", t=2, i=PACK),
                 in_=dn_raw[0][:].rearrange("p i (m t) -> p m i t", t=PACK)[:, :, :, 2 * g : 2 * g + 2],
             )
-        ups = keep.tile([P, N], U8, name="ups", tag="slot_raw0", align_bytes=64)
-        nc.vector.memset(ups[:].bitcast(I32), 0)
-        for r in range(4):
-            nc.sync.dma_start(out=ups[r:128:32, :].bitcast(I32), in_=upw_scales[0, r:16:4, :].bitcast(I32))
         for g in (1, 0):
             quantise_dn(0, 2 * g, dn_bf0[g])
 

@@ -29,6 +29,8 @@ SCALAR_M = 40
 EARLY_BANKS = 3
 Y_BANKS = 3
 LAST_SPLIT = 704
+SM_ROW = P - 1
+B_ROW = P - NT
 
 
 def tile_list_xcross_tanh_kernel(
@@ -48,21 +50,23 @@ def tile_list_xcross_tanh_kernel(
         tabw = keep.tile([P, T], I32, name="tabw", align_bytes=64)
         dn_raw = [keep.tile([P, PACK, R], F32, name="dn_raw0", align_bytes=64)]
         sm_t = keep.tile([P, PACK], F32, name="sm_t")
+        sm_row = keep.tile([P, R], F32, name="sm_row")
         b_rows = keep.tile([P, P], F32, name="b_rows")
         ident = keep.tile([P, P], F32, name="ident")
         planes = keep.tile([P, PASSES * J], U8, name="planes", align_bytes=64)
 
         nc.sync.dma_start(out=tabs[96:128, 0:T].bitcast(I32), in_=tab_scales.bitcast(I32).rearrange("a q t -> q a t"))
         nc.sync.dma_start(offsets[:], offs)
-        nc.scalar.dma_start(out=sm_t[:], in_=sm.rearrange("(p t) -> p t", t=PACK))
         nc.sync.dma_start(out=tabw[:], in_=tab_words[0].rearrange("p t i -> p (t i)").bitcast(I32))
         nc.sync.dma_start(out=dn_raw[0][:], in_=dn[0:512, :].rearrange("(p i) r -> p i r", i=PACK))
 
         nc.vector.memset(tabs[0:96, 0:T].bitcast(I32), 0)
         nc.vector.memset(planes[:].bitcast(I32), 0)
         v_scales = [planes[:, a * J : (a + 1) * J] for a in range(PASSES)]
-        nc.gpsimd.memset(b_rows[:], 0.0)
-        nc.scalar.dma_start(out=b_rows[0:NT, :], in_=b.rearrange("(c p) -> c p", p=P))
+        nc.scalar.dma_start(out=sm_row[SM_ROW:P, :], in_=sm.rearrange("(o r) -> o r", o=1))
+        nc.scalar.dma_start(out=b_rows[B_ROW:P, :], in_=b.rearrange("(c p) -> c p", p=P))
+        nc.gpsimd.memset(sm_row[0:SM_ROW, :], 0.0)
+        nc.gpsimd.memset(b_rows[0:B_ROW, :], 0.0)
         make_identity(nc, ident[:])
 
         picked_rows = keep.tile([P, J], U8, name="picked_rows", align_bytes=64)
@@ -101,6 +105,10 @@ def tile_list_xcross_tanh_kernel(
 
         b_cols = psum.tile([P, HALF], F32, name="b_cols", tag=f"bank{EARLY_BANKS}")
         nc.tensor.transpose(b_cols[:, 0:P], b_rows[:], ident[:])
+        sm_cols = psum.tile([P, PACK, P], F32, name="sm_cols", tag="bank7")
+        for t in range(PACK):
+            nc.tensor.transpose(sm_cols[:, t, :], sm_row[:, t:R:PACK], ident[:])
+        nc.scalar.copy(out=sm_t[:], in_=sm_cols[:, :, SM_ROW])
 
         both, v_codes = [], []
 
@@ -154,7 +162,7 @@ def tile_list_xcross_tanh_kernel(
             )
         quantise_dn(1, 0, dn_bf1)
         b1 = late.tile([P, NT], F32, name="b1", offset=0, align_bytes=64)
-        nc.vector.tensor_scalar(out=b1[:], in0=b_cols[:, 0:NT], scalar1=1.0, scalar2=None, op0=ALU.add)
+        nc.vector.tensor_scalar(out=b1[:], in0=b_cols[:, B_ROW : B_ROW + NT], scalar1=1.0, scalar2=None, op0=ALU.add)
         part_words(1, late.tile([P, PASSES * 2 * HALF], U8, name="v_codes1", offset=64, align_bytes=64))
         load_x0(keep, tag="slot_bf00")
         load_x0(late, offset=64 + PASSES * 2 * HALF)
@@ -201,7 +209,8 @@ def tile_list_xcross_tanh_kernel(
                     quantise_h(pair - 1)
         quantise_h(J // (2 * CH) - 1)
 
-        res = [keep.tile([P, J], F32, name=f"res{c}") for c in range(NT)]
+        res_first = keep.tile([P, 2, J], F32, name="res_first")
+        res = [res_first[:, c, :] for c in range(2)] + [keep.tile([P, J], F32, name=f"res{c}") for c in range(2, NT)]
         y1 = [keep.tile([P, J], F32, name=f"y1_{c}") for c in range(NT)]
         banks_used = []
 
@@ -247,8 +256,7 @@ def tile_list_xcross_tanh_kernel(
             for c in (0, 1):
                 make_y1(c, hh)
                 cross(c, halves[hh])
-                if hh == HALVES - 1:
-                    store(c, whole)
+        nc.sync.dma_start(out=out[0 : 2 * P, :].rearrange("(c p) j -> p c j", p=P), in_=res_first[:])
         for hh in range(HALVES):
             make_y1(2, hh)
         cross(2, whole)

@@ -209,8 +209,8 @@ def tile_list_xcross_tanh_kernel(
                     quantise_h(pair - 1)
         quantise_h(J // (2 * CH) - 1)
 
-        res_first = keep.tile([P, 2, J], F32, name="res_first")
-        res = [res_first[:, c, :] for c in range(2)] + [keep.tile([P, J], F32, name=f"res{c}") for c in range(2, NT)]
+        res_first = keep.tile([P, NT - 1, J], F32, name="res_first")
+        res = [res_first[:, c, :] for c in range(NT - 1)] + [keep.tile([P, J], F32, name="res_last")]
         y1 = [keep.tile([P, J], F32, name=f"y1_{c}") for c in range(NT)]
         banks_used = []
 
@@ -256,11 +256,10 @@ def tile_list_xcross_tanh_kernel(
             for c in (0, 1):
                 make_y1(c, hh)
                 cross(c, halves[hh])
-        nc.sync.dma_start(out=out[0 : 2 * P, :].rearrange("(c p) j -> p c j", p=P), in_=res_first[:])
         for hh in range(HALVES):
             make_y1(2, hh)
         cross(2, whole)
-        store(2, whole)
+        nc.sync.dma_start(out=out[0 : (NT - 1) * P, :].rearrange("(c p) j -> p c j", p=P), in_=res_first[:])
         for hh in range(HALVES):
             make_y1(3, hh)
         for cols in (slice(0, LAST_SPLIT), slice(LAST_SPLIT, J)):

@@ -55,13 +55,13 @@ def tile_list_xcross_tanh_kernel(
         ident = keep.tile([P, P], F32, name="ident")
         planes = keep.tile([P, PASSES * J], U8, name="planes", align_bytes=64)
 
-        nc.sync.dma_start(out=tabs[96:128, 0:T].bitcast(I32), in_=tab_scales.bitcast(I32).rearrange("a q t -> q a t"))
+        nc.sync.dma_start(out=tabs[32:64, 0:T].bitcast(I32), in_=tab_scales.bitcast(I32).rearrange("a q t -> q a t"))
         nc.sync.dma_start(offsets[:], offs)
         nc.sync.dma_start(out=tabw[:], in_=tab_words[0].rearrange("p t i -> p (t i)").bitcast(I32))
         nc.sync.dma_start(out=dn_raw[0][:], in_=dn[0:512, :].rearrange("(p i) r -> p i r", i=PACK))
 
-        nc.vector.memset(tabs[0:96, 0:T].bitcast(I32), 0)
-        nc.vector.memset(planes[:].bitcast(I32), 0)
+        nc.vector.memset(tabs[64:128, 0:T].bitcast(I32), 0)
+        nc.vector.memset(tabs[0:32, 0:T].bitcast(I32), 0)
         v_scales = [planes[:, a * J : (a + 1) * J] for a in range(PASSES)]
         nc.scalar.dma_start(out=sm_row[SM_ROW:P, :], in_=sm.rearrange("(o r) -> o r", o=1))
         nc.scalar.dma_start(out=b_rows[B_ROW:P, :], in_=b.rearrange("(c p) -> c p", p=P))
@@ -77,11 +77,10 @@ def tile_list_xcross_tanh_kernel(
         wbw = reuse.tile([P, PASSES, N], I32, name="wbw", offset=10752, align_bytes=64)
         x0 = [reuse.tile([P, T], F32, name="x0_0", offset=14848, align_bytes=64)]
         wbs, ups = wscales[:, 0 : PASSES * N], wscales[:, PASSES * N :]
-        nc.vector.memset(wscales[:].bitcast(I32), 0)
         for q in (0, 2, 1, 3):
             nc.sync.dma_start(
                 out=planes[32 * q : 32 * q + 4, 0 : PASSES * J].bitcast(I32),
-                in_=picked_rows[96 + 8 * q : 96 + 8 * q + 8, :].bitcast(I32),
+                in_=picked_rows[32 + 8 * q : 32 + 8 * q + 8, :].bitcast(I32),
             )
 
         def load_up_scales(r):

@@ -28,7 +28,7 @@ QUADS = 4
 SCALAR_M = 40
 EARLY_BANKS = 3
 Y_BANKS = 3
-LAST_SPLIT = 704
+LAST_CUTS = (576, 896)
 SM_ROW = P - 1
 B_ROW = P - NT
 
@@ -55,13 +55,12 @@ def tile_list_xcross_tanh_kernel(
         ident = keep.tile([P, P], F32, name="ident")
         planes = keep.tile([P, PASSES * J], U8, name="planes", align_bytes=64)
 
-        nc.sync.dma_start(out=tabs[32:64, 0:T].bitcast(I32), in_=tab_scales.bitcast(I32).rearrange("a q t -> q a t"))
+        nc.sync.dma_start(out=tabs[96:128, 0:T].bitcast(I32), in_=tab_scales.bitcast(I32).rearrange("a q t -> q a t"))
         nc.sync.dma_start(offsets[:], offs)
         nc.sync.dma_start(out=tabw[:], in_=tab_words[0].rearrange("p t i -> p (t i)").bitcast(I32))
         nc.sync.dma_start(out=dn_raw[0][:], in_=dn[0:512, :].rearrange("(p i) r -> p i r", i=PACK))
 
-        nc.vector.memset(tabs[64:128, 0:T].bitcast(I32), 0)
-        nc.vector.memset(tabs[0:32, 0:T].bitcast(I32), 0)
+        nc.vector.memset(tabs[0:96, 0:T].bitcast(I32), 0)
         v_scales = [planes[:, a * J : (a + 1) * J] for a in range(PASSES)]
         nc.scalar.dma_start(out=sm_row[SM_ROW:P, :], in_=sm.rearrange("(o r) -> o r", o=1))
         nc.scalar.dma_start(out=b_rows[B_ROW:P, :], in_=b.rearrange("(c p) -> c p", p=P))
@@ -80,7 +79,7 @@ def tile_list_xcross_tanh_kernel(
         for q in (0, 2, 1, 3):
             nc.sync.dma_start(
                 out=planes[32 * q : 32 * q + 4, 0 : PASSES * J].bitcast(I32),
-                in_=picked_rows[32 + 8 * q : 32 + 8 * q + 8, :].bitcast(I32),
+                in_=picked_rows[96 + 8 * q : 96 + 8 * q + 8, :].bitcast(I32),
             )
 
         def load_up_scales(r):
@@ -261,6 +260,6 @@ def tile_list_xcross_tanh_kernel(
         nc.sync.dma_start(out=out[0 : (NT - 1) * P, :].rearrange("(c p) j -> p c j", p=P), in_=res_first[:])
         for hh in range(HALVES):
             make_y1(3, hh)
-        for cols in (slice(0, LAST_SPLIT), slice(LAST_SPLIT, J)):
+        for cols in (slice(0, LAST_CUTS[0]), slice(*LAST_CUTS), slice(LAST_CUTS[1], J)):
             cross(3, cols)
             store(3, cols)

@@ -18,6 +18,7 @@ ACT = mybir.ActivationFunctionType
 ALU = mybir.AluOpType
 
 P = 128
+BURST = 256
 PACK = 4
 PASSES = K // (P * PACK)
 HALF = 512
@@ -46,14 +47,14 @@ def tile_list_xcross_tanh_kernel(
         reuse = ctx.enter_context(tc.tile_pool(name="reuse", bufs=1))
 
         offsets = keep.tile([P, J // 16], U16, name="offsets")
-        tabs = reuse.tile([P, 6784], U8, name="tabs", offset=8128, align_bytes=64)
-        tabw = keep.tile([P, T], I32, name="tabw", align_bytes=64)
-        dn_raw = [keep.tile([P, PACK, R], F32, name="dn_raw0", align_bytes=64)]
+        tabs = reuse.tile([P, 7168], U8, name="tabs", offset=7936, align_bytes=BURST)
+        tabw = keep.tile([P, T], I32, name="tabw", align_bytes=BURST)
+        dn_raw = [keep.tile([P, PACK, R], F32, name="dn_raw0", align_bytes=BURST)]
         sm_t = keep.tile([P, PACK], F32, name="sm_t")
         sm_row = keep.tile([P, R], F32, name="sm_row")
         b_rows = keep.tile([P, P], F32, name="b_rows")
         ident = keep.tile([P, P], F32, name="ident")
-        planes = keep.tile([P, PASSES * J], U8, name="planes", align_bytes=64)
+        planes = keep.tile([P, PASSES * J], U8, name="planes", align_bytes=BURST)
 
         nc.sync.dma_start(out=tabs[96:128, 0:T].bitcast(I32), in_=tab_scales.bitcast(I32).rearrange("a q t -> q a t"))
         nc.sync.dma_start(offsets[:], offs)
@@ -68,13 +69,13 @@ def tile_list_xcross_tanh_kernel(
         nc.gpsimd.memset(b_rows[0:B_ROW, :], 0.0)
         make_identity(nc, ident[:])
 
-        picked_rows = keep.tile([P, J], U8, name="picked_rows", align_bytes=64)
+        picked_rows = keep.tile([P, J], U8, name="picked_rows", align_bytes=BURST)
         nc.vector.tensor_copy(out=picked_rows[:], in_=tabs[:, 0:T].indirect(offsets[:]))
-        dn_raw.append(reuse.tile([P, PACK, R], F32, name="dn_raw1", offset=0, align_bytes=64))
-        upw = reuse.tile([P, 2 * N], U8, name="upw", offset=8192, align_bytes=64)
-        wscales = reuse.tile([P, (PASSES + 1) * N], U8, name="wscales", offset=9216, align_bytes=64)
-        wbw = reuse.tile([P, PASSES, N], I32, name="wbw", offset=10752, align_bytes=64)
-        x0 = [reuse.tile([P, T], F32, name="x0_0", offset=14848, align_bytes=64)]
+        dn_raw.append(reuse.tile([P, PACK, R], F32, name="dn_raw1", offset=0, align_bytes=BURST))
+        upw = reuse.tile([P, 2 * N], U8, name="upw", offset=8192, align_bytes=BURST)
+        wscales = reuse.tile([P, (PASSES + 1) * N], U8, name="wscales", offset=9216, align_bytes=BURST)
+        wbw = reuse.tile([P, PASSES, N], I32, name="wbw", offset=10752, align_bytes=BURST)
+        x0 = [reuse.tile([P, T], F32, name="x0_0", offset=14848, align_bytes=BURST)]
         wbs, ups = wscales[:, 0 : PASSES * N], wscales[:, PASSES * N :]
         for q in (0, 2, 1, 3):
             nc.sync.dma_start(
@@ -118,7 +119,7 @@ def tile_list_xcross_tanh_kernel(
             )
 
         for hh in range(HALVES):
-            both.append(keep.tile([P, HALF], U32, name=f"both{hh}", tag=f"slot_both{hh}", align_bytes=64))
+            both.append(keep.tile([P, HALF], U32, name=f"both{hh}", tag=f"slot_both{hh}", align_bytes=BURST))
             nc.vector.tensor_copy(
                 out=both[hh][:], in_=tabw[:].bitcast(U32).indirect(offsets[:, hh * HALF // 16 : (hh + 1) * HALF // 16])
             )
@@ -127,7 +128,7 @@ def tile_list_xcross_tanh_kernel(
 
         def load_x0(pool, **place):
             c = len(x0)
-            x0.append(pool.tile([P, T], F32, name=f"x0_{c}", align_bytes=64, **place))
+            x0.append(pool.tile([P, T], F32, name=f"x0_{c}", align_bytes=BURST, **place))
             nc.sync.dma_start(out=x0[c][:], in_=x0T[c * P : (c + 1) * P, :])
 
 
@@ -144,7 +145,7 @@ def tile_list_xcross_tanh_kernel(
 
         dn_bf0 = []
         for g, copy in enumerate((nc.scalar.copy, nc.vector.tensor_copy)):
-            dn_bf0.append(keep.tile([P, 2 * P * PACK], BF16, name=f"dn_bf0{g}", tag=f"slot_bf0{g}", align_bytes=64))
+            dn_bf0.append(keep.tile([P, 2 * P * PACK], BF16, name=f"dn_bf0{g}", tag=f"slot_bf0{g}", align_bytes=BURST))
             copy(
                 out=dn_bf0[g][:].rearrange("p (t m i) -> p m i t", t=2, i=PACK),
                 in_=dn_raw[0][:].rearrange("p i (m t) -> p m i t", t=PACK)[:, :, :, 2 * g : 2 * g + 2],
@@ -163,7 +164,7 @@ def tile_list_xcross_tanh_kernel(
         nc.vector.tensor_scalar(out=b1[:], in0=b_cols[:, B_ROW : B_ROW + NT], scalar1=1.0, scalar2=None, op0=ALU.add)
         part_words(1, late.tile([P, PASSES * 2 * HALF], U8, name="v_codes1", offset=64, align_bytes=64))
         load_x0(keep, tag="slot_bf00")
-        load_x0(late, offset=64 + PASSES * 2 * HALF)
+        load_x0(late, offset=BURST + PASSES * 2 * HALF)
         load_x0(keep, tag="slot_both1")
         h_codes = [keep.tile([P, HALF], U32, name=f"h_codes{hh}", align_bytes=64) for hh in range(HALVES)]
         h_scales = [keep.tile([P, HALF], U8, name=f"h_scales{hh}", align_bytes=64) for hh in range(HALVES)]
@@ -207,8 +208,8 @@ def tile_list_xcross_tanh_kernel(
                     quantise_h(pair - 1)
         quantise_h(J // (2 * CH) - 1)
 
-        res_first = keep.tile([P, NT - 1, J], F32, name="res_first")
-        res = [res_first[:, c, :] for c in range(NT - 1)] + [keep.tile([P, J], F32, name="res_last")]
+        res_first = keep.tile([P, NT - 1, J], F32, name="res_first", align_bytes=BURST)
+        res = [res_first[:, c, :] for c in range(NT - 1)] + [keep.tile([P, J], F32, name="res_last", align_bytes=BURST)]
         y1 = [keep.tile([P, J], F32, name=f"y1_{c}") for c in range(NT)]
         banks_used = []
 

@@ -30,6 +30,7 @@ SCALAR_M = 40
 EARLY_BANKS = 3
 Y_BANKS = 3
 LAST_CUTS = (576, 896)
+FIRST_WORDS = 768
 SM_ROW = P - 1
 B_ROW = P - NT
 
@@ -56,18 +57,21 @@ def tile_list_xcross_tanh_kernel(
         ident = keep.tile([P, P], F32, name="ident")
         planes = keep.tile([P, PASSES * J], U8, name="planes", align_bytes=BURST)
 
-        nc.sync.dma_start(out=tabs[96:128, 0:T].bitcast(I32), in_=tab_scales.bitcast(I32).rearrange("a q t -> q a t"))
+        words = tab_words[0].rearrange("p t i -> p (t i)").bitcast(I32)
+        nc.vector.memset(tabs[:, 0:T].bitcast(I32), 0)
+        nc.sync.dma_start(out=tabw[:, 0:FIRST_WORDS], in_=words[:, 0:FIRST_WORDS])
         nc.sync.dma_start(offsets[:], offs)
-        nc.sync.dma_start(out=tabw[:], in_=tab_words[0].rearrange("p t i -> p (t i)").bitcast(I32))
+        nc.sync.dma_start(out=tabs[0:P:4, 0:T].bitcast(I32), in_=tab_scales.bitcast(I32).rearrange("a q t -> q a t"))
+        nc.sync.dma_start(out=tabw[:, FIRST_WORDS:T], in_=words[:, FIRST_WORDS:T])
         nc.sync.dma_start(out=dn_raw[0][:], in_=dn[0:512, :].rearrange("(p i) r -> p i r", i=PACK))
 
-        nc.vector.memset(tabs[0:96, 0:T].bitcast(I32), 0)
         v_scales = [planes[:, a * J : (a + 1) * J] for a in range(PASSES)]
         nc.scalar.dma_start(out=sm_row[SM_ROW:P, :], in_=sm.rearrange("(o r) -> o r", o=1))
         nc.scalar.dma_start(out=b_rows[B_ROW:P, :], in_=b.rearrange("(c p) -> c p", p=P))
-        nc.gpsimd.memset(sm_row[0:SM_ROW, :], 0.0)
-        nc.gpsimd.memset(b_rows[0:B_ROW, :], 0.0)
-        make_identity(nc, ident[:])
+        nc.vector.memset(ident[:], 0.0)
+        nc.vector.memset(b_rows[0:B_ROW, :], 0.0)
+        nc.vector.memset(sm_row[0:SM_ROW, :], 0.0)
+        make_identity(nc, ident[:], nomemset=True)
 
         picked_rows = keep.tile([P, J], U8, name="picked_rows", align_bytes=BURST)
         nc.vector.tensor_copy(out=picked_rows[:], in_=tabs[:, 0:T].indirect(offsets[:]))
@@ -80,7 +84,7 @@ def tile_list_xcross_tanh_kernel(
         for q in (0, 2, 1, 3):
             nc.sync.dma_start(
                 out=planes[32 * q : 32 * q + 4, 0 : PASSES * J].bitcast(I32),
-                in_=picked_rows[96 + 8 * q : 96 + 8 * q + 8, :].bitcast(I32),
+                in_=picked_rows[32 * q : 32 * (q + 1) : 4, :].bitcast(I32),
             )
 
         def load_up_scales(r):

from contextlib import ExitStack

import concourse.mybir as mybir
from concourse.masks import make_identity

K, R, N, T, J = 1024, 512, 512, 4096, 1024
FLOPS = 2 * J * (K * R + K * N + R * N)

F32 = mybir.dt.float32
BF16 = mybir.dt.bfloat16
I32 = mybir.dt.int32
U32 = mybir.dt.uint32
U16 = mybir.dt.uint16
U8 = mybir.dt.uint8
FP8X4 = mybir.dt.float8_e4m3fn_x4
FP4X4 = mybir.dt.float4_e2m1fn_x4
ACT = mybir.ActivationFunctionType
ALU = mybir.AluOpType

P = 128
BURST = 256
PACK = 4
PASSES = K // (P * PACK)
HALF = 512
HALVES = J // HALF
CH = 128
NT = N // P
QUADS = 4
SCALAR_M = 40
EARLY_BANKS = 3
Y_BANKS = 3
LAST_CUTS = (576, 896)
FIRST_WORDS = 768
SM_ROW = P - 1
B_ROW = P - NT


def tile_list_xcross_tanh_kernel(
    tc, tab_words, tab_scales, wb_words, wb_scales, dn, sm, upw_words, upw_scales, x0T, b, offs, out
):
    nc = tc.nc
    with ExitStack() as ctx:
        keep = ctx.enter_context(tc.tile_pool(name="keep", bufs=1))
        ring = ctx.enter_context(tc.tile_pool(name="ring", bufs=2))
        psum = ctx.enter_context(tc.psum_pool(name="psum", bufs=1))

        late = ctx.enter_context(tc.tile_pool(name="late", bufs=1))
        reuse = ctx.enter_context(tc.tile_pool(name="reuse", bufs=1))

        offsets = keep.tile([P, J // 16], U16, name="offsets")
        tabs = reuse.tile([P, 7168], U8, name="tabs", offset=7936, align_bytes=BURST)
        tabw = keep.tile([P, T], I32, name="tabw", align_bytes=BURST)
        dn_raw = [keep.tile([P, PACK, R], F32, name="dn_raw0", align_bytes=BURST)]
        sm_t = keep.tile([P, PACK], F32, name="sm_t")
        sm_row = keep.tile([P, R], F32, name="sm_row")
        b_rows = keep.tile([P, P], F32, name="b_rows")
        ident = keep.tile([P, P], F32, name="ident")
        planes = keep.tile([P, PASSES * J], U8, name="planes", align_bytes=BURST)

        words = tab_words[0].rearrange("p t i -> p (t i)").bitcast(I32)
        nc.vector.memset(tabs[:, 0:T].bitcast(I32), 0)
        nc.sync.dma_start(out=tabw[:, 0:FIRST_WORDS], in_=words[:, 0:FIRST_WORDS])
        nc.sync.dma_start(offsets[:], offs)
        nc.sync.dma_start(out=tabs[0:P:4, 0:T].bitcast(I32), in_=tab_scales.bitcast(I32).rearrange("a q t -> q a t"))
        nc.sync.dma_start(out=tabw[:, FIRST_WORDS:T], in_=words[:, FIRST_WORDS:T])
        nc.sync.dma_start(out=dn_raw[0][:], in_=dn[0:512, :].rearrange("(p i) r -> p i r", i=PACK))

        v_scales = [planes[:, a * J : (a + 1) * J] for a in range(PASSES)]
        nc.scalar.dma_start(out=sm_row[SM_ROW:P, :], in_=sm.rearrange("(o r) -> o r", o=1))
        nc.scalar.dma_start(out=b_rows[B_ROW:P, :], in_=b.rearrange("(c p) -> c p", p=P))
        nc.vector.memset(ident[:], 0.0)
        nc.vector.memset(b_rows[0:B_ROW, :], 0.0)
        nc.vector.memset(sm_row[0:SM_ROW, :], 0.0)
        make_identity(nc, ident[:], nomemset=True)

        picked_rows = keep.tile([P, J], U8, name="picked_rows", align_bytes=BURST)
        nc.vector.tensor_copy(out=picked_rows[:], in_=tabs[:, 0:T].indirect(offsets[:]))
        dn_raw.append(reuse.tile([P, PACK, R], F32, name="dn_raw1", offset=0, align_bytes=BURST))
        upw = reuse.tile([P, 2 * N], U8, name="upw", offset=8192, align_bytes=BURST)
        wscales = reuse.tile([P, (PASSES + 1) * N], U8, name="wscales", offset=9216, align_bytes=BURST)
        wbw = reuse.tile([P, PASSES, N], I32, name="wbw", offset=10752, align_bytes=BURST)
        x0 = [reuse.tile([P, T], F32, name="x0_0", offset=14848, align_bytes=BURST)]
        wbs, ups = wscales[:, 0 : PASSES * N], wscales[:, PASSES * N :]
        for q in (0, 2, 1, 3):
            nc.sync.dma_start(
                out=planes[32 * q : 32 * q + 4, 0 : PASSES * J].bitcast(I32),
                in_=picked_rows[32 * q : 32 * (q + 1) : 4, :].bitcast(I32),
            )

        def load_up_scales(r):
            nc.sync.dma_start(
                out=wscales[r:128:32, PASSES * N :].bitcast(I32), in_=upw_scales[0, r:16:4, :].bitcast(I32)
            )

        nc.sync.dma_start(out=dn_raw[1][:], in_=dn[512:1024, :].rearrange("(p i) r -> p i r", i=PACK))
        nc.sync.dma_start(out=wbw[:], in_=wb_words.rearrange("a p n i -> p a (n i)").bitcast(I32))
        nc.sync.dma_start(out=upw[:].bitcast(I32), in_=upw_words[0].bitcast(I32))
        for r in (0, 1):
            load_up_scales(r)
        nc.sync.dma_start(out=x0[0][:], in_=x0T[0:P, :])
        for r in range(4):
            nc.sync.dma_start(
                out=wscales[r:128:32, 0 : PASSES * N].bitcast(I32).rearrange("q (a n) -> q a n", a=PASSES),
                in_=wb_scales[:, r:16:4, :].bitcast(I32).rearrange("a q n -> q a n"),
            )
        for r in (2, 3):
            load_up_scales(r)

        b_cols = psum.tile([P, HALF], F32, name="b_cols", tag=f"bank{EARLY_BANKS}")
        nc.tensor.transpose(b_cols[:, 0:P], b_rows[:], ident[:])
        sm_cols = psum.tile([P, PACK, P], F32, name="sm_cols", tag="bank7")
        for t in range(PACK):
            nc.tensor.transpose(sm_cols[:, t, :], sm_row[:, t:R:PACK], ident[:])
        nc.scalar.copy(out=sm_t[:], in_=sm_cols[:, :, SM_ROW])

        both, v_codes = [], []

        def part_words(hh, codes):
            v_codes.append(codes)
            nc.vector.tensor_copy(
                out=v_codes[hh][:].bitcast(U16).rearrange("p (a j) -> p a j", a=PASSES),
                in_=both[hh][:].bitcast(U16).rearrange("p (j a) -> p a j", a=PASSES),
            )

        for hh in range(HALVES):
            both.append(keep.tile([P, HALF], U32, name=f"both{hh}", tag=f"slot_both{hh}", align_bytes=BURST))
            nc.vector.tensor_copy(
                out=both[hh][:], in_=tabw[:].bitcast(U32).indirect(offsets[:, hh * HALF // 16 : (hh + 1) * HALF // 16])
            )
            if hh == 0:
                part_words(0, keep.tile([P, PASSES * 2 * HALF], U8, name="v_codes0", align_bytes=64))

        def load_x0(pool, **place):
            c = len(x0)
            x0.append(pool.tile([P, T], F32, name=f"x0_{c}", align_bytes=BURST, **place))
            nc.sync.dma_start(out=x0[c][:], in_=x0T[c * P : (c + 1) * P, :])


        dn_codes, dn_scales = {}, {}

        def quantise_dn(a, t0, dn_bf):
            width = dn_bf.shape[1] // PACK
            codes = keep.tile([P, width], U32, name=f"dn_codes{a}{t0}", align_bytes=64)
            scales = keep.tile([P, width], U8, name=f"dn_scales{a}{t0}", align_bytes=64)
            nc.vector.quantize_mx(out=codes[:].bitcast(FP8X4), scales=scales[:], in_=dn_bf[:])
            for u in range(width // P):
                dn_codes[a, t0 + u] = codes[:, u * P : (u + 1) * P]
                dn_scales[a, t0 + u] = scales[:, u * P : (u + 1) * P]

        dn_bf0 = []
        for g, copy in enumerate((nc.scalar.copy, nc.vector.tensor_copy)):
            dn_bf0.append(keep.tile([P, 2 * P * PACK], BF16, name=f"dn_bf0{g}", tag=f"slot_bf0{g}", align_bytes=BURST))
            copy(
                out=dn_bf0[g][:].rearrange("p (t m i) -> p m i t", t=2, i=PACK),
                in_=dn_raw[0][:].rearrange("p i (m t) -> p m i t", t=PACK)[:, :, :, 2 * g : 2 * g + 2],
            )
        for g in (1, 0):
            quantise_dn(0, 2 * g, dn_bf0[g])

        dn_bf1 = late.tile([P, PACK * P * PACK], BF16, name="dn_bf1", offset=0, align_bytes=64)
        for copy, ms in ((nc.scalar.copy, slice(0, SCALAR_M)), (nc.vector.tensor_copy, slice(SCALAR_M, P))):
            copy(
                out=dn_bf1[:].rearrange("p (t m i) -> p m i t", t=PACK, i=PACK)[:, ms, :, :],
                in_=dn_raw[1][:].rearrange("p i (m t) -> p m i t", t=PACK)[:, ms, :, :],
            )
        quantise_dn(1, 0, dn_bf1)
        b1 = late.tile([P, NT], F32, name="b1", offset=0, align_bytes=64)
        nc.vector.tensor_scalar(out=b1[:], in0=b_cols[:, B_ROW : B_ROW + NT], scalar1=1.0, scalar2=None, op0=ALU.add)
        part_words(1, late.tile([P, PASSES * 2 * HALF], U8, name="v_codes1", offset=64, align_bytes=64))
        load_x0(keep, tag="slot_bf00")
        load_x0(late, offset=BURST + PASSES * 2 * HALF)
        load_x0(keep, tag="slot_both1")
        h_codes = [keep.tile([P, HALF], U32, name=f"h_codes{hh}", align_bytes=64) for hh in range(HALVES)]
        h_scales = [keep.tile([P, HALF], U8, name=f"h_scales{hh}", align_bytes=64) for hh in range(HALVES)]
        h_bf = []

        def quantise_h(pair):
            hh, part = divmod(pair, 2)
            cols = slice(part * 2 * CH, (part + 1) * 2 * CH)
            nc.vector.quantize_mx(
                out=h_codes[hh][:, cols].bitcast(FP8X4), scales=h_scales[hh][:, cols], in_=h_bf[pair][:]
            )

        for bank in range(J // CH):
            pair, u = divmod(bank, 2)
            j0 = bank * CH
            if u == 0:
                h_bf.append(ring.tile([P, 2 * CH * PACK], BF16, name="h_bf", align_bytes=64))
                th = ring.tile([P, 2 * CH, PACK], F32, name="th", bufs=3)
            hs = psum.tile([P, PACK, CH], F32, name="hs", tag=f"bank{bank}")
            for a in range(PASSES):
                for k, t in enumerate((2, 3, 0, 1)):
                    nc.tensor.matmul_mx(
                        out=hs[:, t, :],
                        lhsT=dn_codes[a, t].bitcast(FP8X4),
                        lhsT_scale=dn_scales[a, t],
                        rhs=v_codes[j0 // HALF][:, 2 * (a * HALF + j0 % HALF) : 2 * (a * HALF + j0 % HALF + CH)].bitcast(FP4X4),
                        rhs_scale=v_scales[a][:, j0 : j0 + CH],
                        start=(a == 0 and k == 0),
                        stop=(a == PASSES - 1 and k == PACK - 1),
                    )
            nc.scalar.activation(out=th[:, u * CH : (u + 1) * CH, :], in_=hs[:].rearrange("p t j -> p j t"), func=ACT.Tanh)
            if pair == 0 or u == 1:
                js = slice(u * CH, (u + 1) * CH) if pair == 0 else slice(0, 2 * CH)
                nc.vector.tensor_tensor(
                    out=h_bf[pair][:].rearrange("p (j t) -> p j t", t=PACK)[:, js, :],
                    in0=th[:, js, :],
                    in1=sm_t[:].unsqueeze(1).to_broadcast([P, js.stop - js.start, PACK]),
                    op=ALU.mult,
                )
                if pair > 0:
                    quantise_h(pair - 1)
        quantise_h(J // (2 * CH) - 1)

        res_first = keep.tile([P, NT - 1, J], F32, name="res_first", align_bytes=BURST)
        res = [res_first[:, c, :] for c in range(NT - 1)] + [keep.tile([P, J], F32, name="res_last", align_bytes=BURST)]
        y1 = [keep.tile([P, J], F32, name=f"y1_{c}") for c in range(NT)]
        banks_used = []

        def make_y1(c, hh):
            cols = slice(hh * HALF, (hh + 1) * HALF)
            y = psum.tile([P, HALF], F32, name="y", tag=f"bank{len(banks_used) % Y_BANKS}")
            banks_used.append(y)
            for a in range(PASSES):
                nc.tensor.matmul_mx(
                    out=y[:],
                    lhsT=wbw[:, a, c * P : (c + 1) * P].bitcast(FP8X4),
                    lhsT_scale=wbs[:, a * N + c * P : a * N + (c + 1) * P],
                    rhs=v_codes[hh][:, 2 * a * HALF : 2 * (a + 1) * HALF].bitcast(FP4X4),
                    rhs_scale=v_scales[a][:, cols],
                    start=(a == 0),
                    stop=False,
                )
            nc.tensor.matmul_mx(
                out=y[:],
                lhsT=upw[:, 2 * c * P : 2 * (c + 1) * P].bitcast(FP4X4),
                lhsT_scale=ups[:, c * P : (c + 1) * P],
                rhs=h_codes[hh][:].bitcast(FP8X4),
                rhs_scale=h_scales[hh][:],
                start=False,
                stop=True,
            )
            nc.scalar.activation(out=y1[c][:, cols], in_=y[:], func=ACT.Identity, bias=b1[:, c : c + 1])

        def cross(c, cols):
            nc.vector.tensor_tensor(
                out=res[c][:, cols],
                in0=x0[c][:].indirect(offsets[:, cols.start // 16 : cols.stop // 16]),
                in1=y1[c][:, cols],
                op=ALU.mult,
            )

        def store(c, cols):
            nc.sync.dma_start(out=out[c * P : (c + 1) * P, cols], in_=res[c][:, cols])

        halves = [slice(hh * HALF, (hh + 1) * HALF) for hh in range(HALVES)]
        whole = slice(0, J)
        for hh in range(HALVES):
            for c in (0, 1):
                make_y1(c, hh)
                cross(c, halves[hh])
        for hh in range(HALVES):
            make_y1(2, hh)
        cross(2, whole)
        nc.sync.dma_start(out=out[0 : (NT - 1) * P, :].rearrange("(c p) j -> p c j", p=P), in_=res_first[:])
        for hh in range(HALVES):
            make_y1(3, hh)
        for cols in (slice(0, LAST_CUTS[0]), slice(*LAST_CUTS), slice(LAST_CUTS[1], J)):
            cross(3, cols)
            store(3, cols)
